import numpy as np
CORES = [1,2,5,7,57,58,61,63,73,74,77,79]
N = 12
W = 1024
def setup_inputs(rng):
    amp = 0.5 + 1.5 * rng.random((2, N, 128, 1), dtype=np.float32)
    return {"u": amp[0] * rng.standard_normal((N, 128, W), dtype=np.float32), "b": amp[1] * rng.standard_normal((N, 128, W), dtype=np.float32)}
def setup_inputs_big(rng):
    d = setup_inputs(rng)
    for k in ("u", "b"): d[k] = (d[k].astype(np.float32) * 1024.0).astype(d[k].dtype)
    return d
def setup_inputs_small(rng):
    d = setup_inputs(rng)
    for k in ("u", "b"): d[k] = (d[k].astype(np.float32) * (1 / 1024.0)).astype(d[k].dtype)
    return d
def setup_inputs_apart(rng):
    d = setup_inputs(rng)
    f = (10.0 ** rng.permutation(np.linspace(-1.5, 1.5, N))).astype(np.float32).reshape(N, 1, 1)
    for k in ("u", "b"): d[k] = (d[k].astype(np.float32) * f).astype(d[k].dtype)
    return d
def reference(u, b):
    g = np.concatenate(list(u.astype(np.float64)), axis=1); bb = np.concatenate(list(b.astype(np.float64)), axis=1)
    p = np.concatenate([g[:, -2:], g, g[:, :2]], axis=1)
    n = 0.125 * (p[:, :-4] + p[:, 1:-3] + p[:, 3:-1] + p[:, 4:]) + 0.5 * bb
    d = n - g
    s = np.stack([(d ** 2).mean(axis=1), np.abs(d).max(axis=1)], axis=1)
    return {"y": np.stack([n[:, W * r:W * r + W] for r in range(N)]).astype(np.float32), "s": np.broadcast_to(s.astype(np.float32), (N, 128, 2))}

@@ -1,0 +1,346 @@
+from concourse.bass import DstId, RemoteDMATransfer
+from concourse.mybir import AluOpType
+
+NR = 12
+WD = 1024
+CHUNKS = [(256, 256), (512, 256), (0, 256), (768, 128), (896, 128)]
+TPOFF = [0, 256, 0, 256, 0]
+USEQ = [True, False, False, False, False]
+DPASS = [False, False, False, False, False]
+ANYD = any(DPASS)
+ZW = 256 if ANYD else 128
+NEV = 120
+
+SCRATCH = {
+    "X": ("sbuf", [128, 1028], "float32"), "B": ("sbuf", [128, 1024], "float32"),
+    "P": ("sbuf", [128, 1028], "float32"), "Q": ("sbuf", [128, 1024], "float32"),
+    "EB": ("sbuf", [128, 4], "float32"), "RB": ("sbuf", [128, 8], "float32"),
+    "ZT": ("sbuf", [128, ZW + 2], "float32"), "ZN": ("sbuf", [128, 129], "float32"),
+    "I8": ("sbuf", [128, 128], "float32"), "I2": ("sbuf", [128, 128], "float32"), "IN": ("sbuf", [128, 128], "float32"),
+    "CV": ("sbuf", [128, 2], "float32"),
+    "DS": ("sbuf", [128, 1024], "float32"), "NSQ": ("sbuf", [128, 1024], "float32"),
+    "AB": ("sbuf", [128, 1024], "float32"), "Y": ("sbuf", [128, 1024], "float32"),
+    "FS": ("sbuf", [128, 128], "float32"), "FM": ("sbuf", [128, 128], "float32"),
+    "GS": ("sbuf", [128, 128], "float32"), "GM2": ("sbuf", [128, 64], "float32"),
+    "HM": ("sbuf", [128, 64], "float32"), "TR": ("sbuf", [128, 64], "float32"),
+    "TS": ("sbuf", [128, 128], "float32"),
+    "L1": ("sbuf", [128, 16], "float32"), "L2": ("sbuf", [128, 12], "float32"),
+    "A8": ("sbuf", [128, 8], "float32"), "M8": ("sbuf", [128, 8], "float32"),
+    "A4": ("sbuf", [128, 4], "float32"), "M4": ("sbuf", [128, 4], "float32"),
+    "M4B": ("sbuf", [128, 4], "float32"), "WB": ("sbuf", [128, 4], "float32"),
+    "D8": ("dram", [16512], "float32"), "D2": ("dram", [16512], "float32"), "DN": ("dram", [16512], "float32"),
+    "Y0": ("psum", [128, 512], "float32"), "Y1": ("psum", [128, 512], "float32"),
+    "Y2": ("psum", [128, 512], "float32"), "Y3": ("psum", [128, 512], "float32"),
+    "Y4": ("psum", [128, 512], "float32"), "TP": ("psum", [128, 512], "float32"),
+    "ACC": ("psum", [128, 512], "float32"), "MP": ("psum", [128, 512], "float32"),
+}
+SEMAPHORES = (["le", "ms", "ms2", "zd", "li", "hl", "hr", "a1", "a2", "ls", "ys", "ss",
+               "rl0", "rl1", "rl2", "rl3", "lu0", "lu1", "lu2", "lu3", "lb0", "lb1", "lb2", "lb3"]
+              + ["e%d" % i for i in range(NEV)])
+
+
+def rank_program(g, core, T, topo):
+    rank = T.rank_of(core)
+    if rank is None:
+        return
+    V, PE, SY, SC, S = g.vector, g.tensor, g.sync, g.scalar, T.sem
+    ADD, SUB, MUL, MAX = AluOpType.add, AluOpType.subtract, AluOpType.mult, AluOpType.max
+    cores = list(T.cores)
+    n = len(cores)
+    nev = [0]
+    lsn = [0]
+
+    def ev():
+        s = S["e%d" % nev[0]]
+        nev[0] += 1
+        return s
+
+    def pc(m):
+        return bin(m).count("1")
+
+    def relay_for(src, dst):
+        if topo.may_write(src, dst):
+            return None
+        cand = [c for c in cores if c != src and c != dst and topo.chip(c) == topo.chip(src) and topo.may_write(c, dst)]
+        same = [c for c in cand if topo.die(c) == topo.die(dst)]
+        return (same or cand)[0]
+
+    halo = []
+    for r in range(n):
+        halo.append((cores[r], cores[(r - 1) % n], "R", relay_for(cores[r], cores[(r - 1) % n])))
+        halo.append((cores[r], cores[(r + 1) % n], "L", relay_for(cores[r], cores[(r + 1) % n])))
+    jobs = [h for h in halo if h[3] is not None]
+
+    chips = sorted(set(topo.chip(c) for c in cores))
+    plan = {}
+    for ch in chips:
+        mine = [c for c in cores if topo.chip(c) == ch]
+        load = dict((c, 0) for c in mine)
+        dsts = [d for d in cores if topo.chip(d) != ch]
+        dsts.sort(key=lambda d: sum(1 for c in mine if topo.may_write(c, d)))
+        for d in dsts:
+            el = [c for c in mine if topo.may_write(c, d)]
+            best = min(el, key=lambda c: (load[c], topo.die(c) != topo.die(d)))
+            load[best] += 1
+            plan.setdefault(best, []).append(d)
+    peers = [c for c in cores if topo.chip(c) == topo.chip(core)]
+    me = peers.index(core)
+
+    def send(dst, out_ap, in_ap, rsem):
+        rid, pid, _ = topo.addr(dst)
+        m = topo.mask(core, dst)
+        g.remote_dma(out_ap=out_ap, in_ap=in_ap, remote_sem=rsem, local_sem=S.ls, pid=pid, routing_id=rid,
+                     dma_engine_mask=m)
+        lsn[0] += pc(m)
+
+    def fused(dsts, src, dst_aps, rsem):
+        m = topo.mask(core, dsts[0])
+        for d in dsts:
+            m &= topo.mask(core, d)
+        ids = [DstId(rid=topo.addr(d)[0], pnc=topo.addr(d)[1]) for d in dsts]
+        g.remote_dma_fused([RemoteDMATransfer(dst_ids=ids, dma_engine_mask=m, remote_sem=rsem, srcs=[src],
+                                              dsts=dst_aps, alu_op=0)], local_sem=S.ls)
+        lsn[0] += pc(m)
+
+    def halo_ap(side):
+        return (T.X[:, 1026:1028], S.hr) if side == "R" else (T.X[:, 0:2], S.hl)
+
+    SY.dma_start(T.EB[:, 0:2], T.u[:, 0:2]).then_inc(S.le, 16)
+    SY.dma_start(T.EB[:, 2:4], T.u[:, 1022:1024]).then_inc(S.le, 16)
+    for i, (a, b) in enumerate([(252, 516), (516, 772), (0, 252), (772, 1024)]):
+        SY.dma_start(T.X[:, a + 2:b + 2], T.u[:, a:b]).then_inc(S["lu%d" % i], 16)
+
+    nms = 3
+    V.memset(T.ZT[:, 0:1], 0.125).then_inc(S.ms, 1)
+    V.memset(T.ZT[:, 1:ZW + 1], 0.0).then_inc(S.ms, 1)
+    V.memset(T.ZT[:, ZW + 1:ZW + 2], 0.5).then_inc(S.ms, 1)
+    if ANYD:
+        V.memset(T.ZN[:, 0:1], -1.0).then_inc(S.ms, 1)
+        V.memset(T.ZN[:, 1:129], 0.0).then_inc(S.ms, 1)
+        nms = 5
+    V.memset(T.CV[:, 0:1], 0.0).then_inc(S.ms2, 1)
+    V.memset(T.CV[:, 1:2], -8.0 / (NR * WD)).then_inc(S.ms2, 1)
+
+    SC.wait_ge(S.ms, nms)
+    SC.dma_start(T.D8[:], T.ZT[:, 0:129]).then_inc(S.zd, 16)
+    SC.dma_start(T.D2[:], T.ZT[:, ZW - 127:ZW + 2]).then_inc(S.zd, 16)
+    nI = 2
+    if ANYD:
+        SC.dma_start(T.DN[:], T.ZN[:, 0:129]).then_inc(S.zd, 16)
+        nI = 3
+    SC.dma_start(T.B[:, 256:512], T.b[:, 256:512]).then_inc(S.lb0, 16)
+    SC.dma_start(T.B[:, 512:768], T.b[:, 512:768]).then_inc(S.lb1, 16)
+    SC.wait_ge(S.zd, 16 * nI)
+    SC.dma_start(T.I8[:, :], T.D8[0:16384]).then_inc(S.li, 16)
+    SC.dma_start(T.I2[:, :], T.D2[128:16512]).then_inc(S.li, 16)
+    if ANYD:
+        SC.dma_start(T.IN[:, :], T.DN[0:16384]).then_inc(S.li, 16)
+    SC.dma_start(T.B[:, 0:256], T.b[:, 0:256]).then_inc(S.lb2, 16)
+    SC.dma_start(T.B[:, 768:1024], T.b[:, 768:1024]).then_inc(S.lb3, 16)
+    lbsem = [S.lb0, S.lb1, S.lb2, S.lb3, S.lb3]
+
+    g.wait_ge(S.le, 32)
+    mysends = [h for h in halo if h[0] == core]
+    mysends.sort(key=lambda h: (h[3] is None, topo.chip(h[1]) == topo.chip(core)))
+    for h in mysends:
+        src_ap = T.EB[:, 0:2] if h[2] == "R" else T.EB[:, 2:4]
+        if h[3] is None:
+            ap, sem = halo_ap(h[2])
+            send(h[1], ap, src_ap, sem)
+        else:
+            j = jobs.index(h)
+            send(h[3], T.RB[:, 2 * j:2 * j + 2], src_ap, S["rl%d" % j])
+    for j, h in enumerate(jobs):
+        if h[3] == core:
+            g.wait_ge(S["rl%d" % j], pc(topo.mask(h[0], core)))
+            ap, sem = halo_ap(h[2])
+            send(h[1], ap, T.RB[:, 2 * j:2 * j + 2], sem)
+    hcount = {}
+    for h in halo:
+        if h[1] == core:
+            hcount[h[2]] = pc(topo.mask(h[0] if h[3] is None else h[3], core))
+
+    pev = {}
+
+    def pairs(name, j0, j1):
+        pev[name] = ev()
+        V.tensor_tensor(T.P[:, j0:j1], T.X[:, j0:j1], T.X[:, j0 + 1:j1 + 1], ADD).then_inc(pev[name], 1)
+
+    pdeps = [["A"], ["A", "B"], ["L", "C", "A"], ["B", "D"], ["D", "R"]]
+    qev = {}
+    V.wait_ge(S.lu0, 16)
+    pairs("A", 254, 517)
+    if USEQ[0]:
+        c0, w = CHUNKS[0]
+        qev[0] = ev()
+        V.wait_ge(pev["A"], 1)
+        V.tensor_tensor(T.Q[:, c0:c0 + w], T.P[:, c0:c0 + w], T.P[:, c0 + 3:c0 + 3 + w], ADD).then_inc(qev[0], 1)
+    V.wait_ge(S.lu1, 16)
+    pairs("B", 517, 773)
+    V.wait_ge(S.lu2, 16)
+    pairs("C", 2, 254)
+    V.wait_ge(S.lu3, 16)
+    pairs("D", 773, 1025)
+    if ANYD:
+        V.wait_ge(S.ms, nms)
+
+    evY = [ev() for _ in CHUNKS]
+    eGS, eT, eTS, eO = ev(), ev(), ev(), ev()
+
+    accS, accM = T.ACC[:, 0:256], T.ACC[:, 256:512]
+    prev = None
+    for k, (c0, w) in enumerate(CHUNKS):
+        Yk = T["Y%d" % k][:, 0:w]
+        Xc = T.X[:, c0 + 2:c0 + 2 + w]
+        ds = T.DS[:, c0:c0 + w]
+        V.wait_ge(evY[k], 1)
+        e1 = ev()
+        if DPASS[k]:
+            ps = Yk
+            V.tensor_tensor(ds, T.ZT[:, 1:1 + w], Yk, SUB).then_inc(e1, 1)
+            V.wait_ge(e1, 1)
+        else:
+            ps = T.TP[:, TPOFF[k]:TPOFF[k] + w]
+            V.tensor_tensor(ds, Yk, Xc, SUB).then_inc(e1, 1)
+            V.tensor_tensor(ps, Xc, Yk, SUB).then_inc(e1, 1)
+            V.wait_ge(e1, 2)
+        e2 = ev()
+        if k == 0:
+            os_, om = T.ACC[:, 0:w], T.ACC[:, 256:256 + w]
+        else:
+            os_, om = T.NSQ[:, c0:c0 + w], T.AB[:, c0:c0 + w]
+        V.tensor_tensor(os_, ps, ds, MUL).then_inc(e2, 1)
+        V.tensor_tensor(om, ps, ds, MAX).then_inc(e2, 1)
+        V.wait_ge(e2, 2)
+        if k == 0:
+            prev = e2
+            V.wait_ge(S.hl, hcount["L"])
+            pairs("L", 0, 2)
+        elif k < 4:
+            V.wait_ge(prev, 2)
+            e3 = ev()
+            V.tensor_tensor(T.ACC[:, 0:w], T.ACC[:, 0:w], os_, ADD).then_inc(e3, 1)
+            V.tensor_tensor(T.ACC[:, 256:256 + w], T.ACC[:, 256:256 + w], om, MAX).then_inc(e3, 1)
+            prev = e3
+            if k == 1:
+                V.wait_ge(S.hr, hcount["R"])
+                pairs("R", 1025, 1027)
+        else:
+            V.wait_ge(prev, 2)
+            e3 = ev()
+            V.tensor_tensor(T.FS[:, :], T.ACC[:, 128:256], os_, ADD).then_inc(e3, 1)
+            V.tensor_tensor(T.FM[:, :], T.ACC[:, 384:512], om, MAX).then_inc(e3, 1)
+            V.wait_ge(e3, 2)
+    V.tensor_tensor(T.GS[:, :], T.ACC[:, 0:128], T.FS[:, :], ADD).then_inc(eGS, 1)
+    e4 = ev()
+    V.tensor_tensor(T.TP[:, 384:448], T.ACC[:, 256:320], T.FM[:, 0:64], MAX).then_inc(e4, 1)
+    V.tensor_tensor(T.GM2[:, :], T.ACC[:, 320:384], T.FM[:, 64:128], MAX).then_inc(e4, 1)
+    V.wait_ge(e4, 2)
+    e5 = ev()
+    V.tensor_tensor(T.HM[:, :], T.TP[:, 384:448], T.GM2[:, :], MAX).then_inc(e5, 1)
+    V.wait_ge(e5, 1)
+    e6 = ev()
+    V.tensor_tensor(T.TR[:, 0:32], T.HM[:, 0:32], T.HM[:, 32:64], MAX).then_inc(e6, 1)
+    V.wait_ge(eT, 1)
+    V.tensor_copy(T.TS[:, :], T.MP[:, 0:128]).then_inc(eTS, 1)
+    slot = T.L1[:, 4 * me:4 * me + 4]
+    eMSG = ev()
+    lo, wd, last = 0, 32, e6
+    while wd > 2:
+        h = wd // 2
+        V.wait_ge(last, 1)
+        if h == 2:
+            V.tensor_tensor(T.L1[:, 4 * me + 2:4 * me + 4], T.TR[:, lo:lo + h], T.TR[:, lo + h:lo + wd], MAX).then_inc(eMSG, 1)
+        else:
+            last = ev()
+            V.tensor_tensor(T.TR[:, lo + wd:lo + wd + h], T.TR[:, lo:lo + h], T.TR[:, lo + h:lo + wd], MAX).then_inc(last, 1)
+        lo += wd
+        wd = h
+    V.wait_ge(eO, 1)
+    V.tensor_copy(T.L1[:, 4 * me:4 * me + 2], T.MP[:, 128:130]).then_inc(eMSG, 1)
+
+    PE.wait_ge(S.li, 16 * nI)
+    for k, (c0, w) in enumerate(CHUNKS):
+        out = T["Y%d" % k][:, 0:w]
+        taps = []
+        if USEQ[k]:
+            PE.wait_ge(qev[k], 1)
+            taps.append((T.I8, T.Q[:, c0:c0 + w]))
+        else:
+            for nm in pdeps[k]:
+                PE.wait_ge(pev[nm], 1)
+            taps.append((T.I8, T.P[:, c0:c0 + w]))
+            taps.append((T.I8, T.P[:, c0 + 3:c0 + 3 + w]))
+        if DPASS[k]:
+            taps.append((T.IN, T.X[:, c0 + 2:c0 + 2 + w]))
+        for i, (m, r) in enumerate(taps):
+            PE.matmul(out, m[:, :], r, i == 0, False)
+        PE.wait_ge(lbsem[k], 16)
+        PE.matmul(out, T.I2[:, :], T.B[:, c0:c0 + w], False, True).then_inc(evY[k], 1)
+    PE.wait_ge(eGS, 1)
+    PE.matmul(T.MP[:, 0:128], T.GS[:, :], T.I8[:, :], True, True).then_inc(eT, 1)
+    PE.wait_ge(S.ms2, 2)
+    PE.wait_ge(eTS, 1)
+    PE.matmul(T.MP[:, 128:130], T.TS[:, :], T.CV[:, :], True, True).then_inc(eO, 1)
+
+    others = [c for c in peers if c != core]
+    g.wait_ge(eMSG, 2)
+    fused(others, slot, [slot for _ in others], S.a1)
+
+    yev = []
+
+    def yout(k):
+        c0, w = CHUNKS[k]
+        e = ev()
+        yev.append((k, e))
+        if DPASS[k]:
+            V.tensor_tensor(T.Y[:, c0:c0 + w], T["Y%d" % k][:, 0:w], T.X[:, c0 + 2:c0 + 2 + w], ADD).then_inc(e, 1)
+        else:
+            V.tensor_copy(T.Y[:, c0:c0 + w], T["Y%d" % k][:, 0:w]).then_inc(e, 1)
+
+    for k in (0, 1, 2):
+        yout(k)
+    V.wait_ge(eMSG, 2)
+    V.wait_ge(S.a1, sum(pc(topo.mask(c, core)) for c in others))
+    e7 = ev()
+    V.tensor_tensor(T.A8[:, :], T.L1[:, 0:8], T.L1[:, 8:16], ADD).then_inc(e7, 1)
+    V.tensor_tensor(T.M8[:, :], T.L1[:, 0:8], T.L1[:, 8:16], MAX).then_inc(e7, 1)
+    V.wait_ge(e7, 2)
+    eC = ev()
+    V.tensor_tensor(T.L2[:, 0:2], T.A8[:, 0:2], T.A8[:, 4:6], ADD).then_inc(eC, 1)
+    V.tensor_tensor(T.L2[:, 2:4], T.M8[:, 2:4], T.M8[:, 6:8], MAX).then_inc(eC, 1)
+
+    def slot2(src_chip, dst):
+        oth = [x for x in chips if x != topo.chip(dst)]
+        i = 1 + oth.index(src_chip)
+        return T.L2[:, 4 * i:4 * i + 4]
+
+    if core in plan:
+        g.wait_ge(eC, 2)
+        fused(plan[core], T.L2[:, 0:4], [slot2(topo.chip(core), d) for d in plan[core]], S.a2)
+    g.wait_ge(S.ls, lsn[0])
+
+    for k in (3, 4):
+        yout(k)
+    na2 = sum(pc(topo.mask(s, core)) for s in plan for d in plan[s] if d == core)
+    V.wait_ge(eC, 2)
+    V.wait_ge(S.a2, na2)
+    e8 = ev()
+    V.tensor_tensor(T.A4[:, :], T.L2[:, 0:4], T.L2[:, 4:8], ADD).then_inc(e8, 1)
+    V.tensor_tensor(T.M4[:, :], T.L2[:, 0:4], T.L2[:, 4:8], MAX).then_inc(e8, 1)
+    V.wait_ge(e8, 2)
+    e9 = ev()
+    V.tensor_tensor(T.WB[:, :], T.A4[:, :], T.L2[:, 8:12], ADD).then_inc(e9, 1)
+    V.tensor_tensor(T.M4B[:, :], T.M4[:, :], T.L2[:, 8:12], MAX).then_inc(e9, 1)
+    V.wait_ge(e9, 2)
+    eS = ev()
+    V.tensor_tensor(T.WB[:, 2:3], T.M4B[:, 2:3], T.M4B[:, 3:4], MAX).then_inc(eS, 1)
+
+    for k, e in yev:
+        c0, w = CHUNKS[k]
+        SC.wait_ge(e, 1)
+        SC.dma_start(T.y[:, c0:c0 + w], T.Y[:, c0:c0 + w]).then_inc(S.ys, 16)
+    SC.wait_ge(S.ys, 16 * len(yev))
+    SY.wait_ge(eS, 1)
+    SY.dma_start(T.s[:, :], T.WB[:, 1:3]).then_inc(S.ss, 16)
+    SY.wait_ge(S.ss, 16)

@@ -3,19 +3,14 @@ from concourse.mybir import AluOpType
 
 NR = 12
 WD = 1024
-CHUNKS = [(256, 256), (512, 256), (0, 256), (768, 128), (896, 128)]
-TPOFF = [0, 256, 0, 256, 0]
-USEQ = [True, False, False, False, False]
-DPASS = [False, False, False, False, False]
-ANYD = any(DPASS)
-ZW = 256 if ANYD else 128
+H0, H1 = 384, 640
 NEV = 120
 
 SCRATCH = {
     "X": ("sbuf", [128, 1028], "float32"), "B": ("sbuf", [128, 1024], "float32"),
     "P": ("sbuf", [128, 1028], "float32"), "Q": ("sbuf", [128, 1024], "float32"),
     "EB": ("sbuf", [128, 4], "float32"), "RB": ("sbuf", [128, 8], "float32"),
-    "ZT": ("sbuf", [128, ZW + 2], "float32"), "ZN": ("sbuf", [128, 129], "float32"),
+    "ZT": ("sbuf", [128, 130], "float32"), "ZN": ("sbuf", [128, 129], "float32"),
     "I8": ("sbuf", [128, 128], "float32"), "I2": ("sbuf", [128, 128], "float32"), "IN": ("sbuf", [128, 128], "float32"),
     "CV": ("sbuf", [128, 2], "float32"),
     "DS": ("sbuf", [128, 1024], "float32"), "NSQ": ("sbuf", [128, 1024], "float32"),
@@ -24,29 +19,40 @@ SCRATCH = {
     "GS": ("sbuf", [128, 128], "float32"), "GM2": ("sbuf", [128, 64], "float32"),
     "HM": ("sbuf", [128, 64], "float32"), "TR": ("sbuf", [128, 64], "float32"),
     "TS": ("sbuf", [128, 128], "float32"),
-    "L1": ("sbuf", [128, 16], "float32"), "L2": ("sbuf", [128, 12], "float32"),
+    "L1": ("sbuf", [128, 32], "float32"), "L2": ("sbuf", [128, 12], "float32"),
+    "A16": ("sbuf", [128, 16], "float32"), "M16": ("sbuf", [128, 16], "float32"),
     "A8": ("sbuf", [128, 8], "float32"), "M8": ("sbuf", [128, 8], "float32"),
     "A4": ("sbuf", [128, 4], "float32"), "M4": ("sbuf", [128, 4], "float32"),
     "M4B": ("sbuf", [128, 4], "float32"), "WB": ("sbuf", [128, 4], "float32"),
     "D8": ("dram", [16512], "float32"), "D2": ("dram", [16512], "float32"), "DN": ("dram", [16512], "float32"),
     "Y0": ("psum", [128, 512], "float32"), "Y1": ("psum", [128, 512], "float32"),
     "Y2": ("psum", [128, 512], "float32"), "Y3": ("psum", [128, 512], "float32"),
-    "Y4": ("psum", [128, 512], "float32"), "TP": ("psum", [128, 512], "float32"),
+    "TP": ("psum", [128, 512], "float32"),
     "ACC": ("psum", [128, 512], "float32"), "MP": ("psum", [128, 512], "float32"),
 }
-SEMAPHORES = (["le", "ms", "ms2", "zd", "li", "hl", "hr", "a1", "a2", "ls", "ys", "ss",
-               "rl0", "rl1", "rl2", "rl3", "lu0", "lu1", "lu2", "lu3", "lb0", "lb1", "lb2", "lb3"]
+SEMAPHORES = (["le", "ms", "ms2", "zd", "li", "hl", "hr", "a1", "a2", "ls", "ys", "ss", "hx", "hb", "yh", "lbh",
+               "rl0", "rl1", "rl2", "rl3", "lu0", "lu1", "lu2", "lu3", "lu4", "lb0", "lb1", "lb2", "lb3"]
               + ["e%d" % i for i in range(NEV)])
 
 
 def rank_program(g, core, T, topo):
-    rank = T.rank_of(core)
-    if rank is None:
+    cores = list(T.cores)
+    n = len(cores)
+    chips = sorted(set(topo.chip(c) for c in cores))
+    helper = {}
+    for ch in chips:
+        mine = [c for c in cores if topo.chip(c) == ch]
+        idle = [c for c in range(max(0, min(mine) - 8), max(mine) + 8) if topo.chip(c) == ch and c not in cores]
+        for c in mine:
+            same = [i for i in idle if topo.die(i) == topo.die(c)]
+            helper[c] = (same or idle)[0]
+            idle.remove(helper[c])
+    owner = dict((h, c) for c, h in helper.items())
+    isr = core in helper
+    if not isr and core not in owner:
         return
     V, PE, SY, SC, S = g.vector, g.tensor, g.sync, g.scalar, T.sem
     ADD, SUB, MUL, MAX = AluOpType.add, AluOpType.subtract, AluOpType.mult, AluOpType.max
-    cores = list(T.cores)
-    n = len(cores)
     nev = [0]
     lsn = [0]
 
@@ -57,6 +63,26 @@ def rank_program(g, core, T, topo):
 
     def pc(m):
         return bin(m).count("1")
+
+    if isr:
+        CH = [(128, 256), (640, 256), (0, 128), (896, 128)]
+        USEQ = [True, False, False, False]
+        DP = [False, False, False, False]
+        pdeps = [["A"], ["B"], ["L", "C", "A"], ["B", "D", "R"]]
+        lbs = [(S.lb0, 16), (S.lb1, 16), (S.lb2, 16), (S.lb3, 16)]
+    else:
+        CH = [(384, 128), (512, 128)]
+        USEQ = [False, False]
+        DP = [True, True]
+        pdeps = [["A"], ["A", "B"]]
+        nhb = pc(topo.mask(owner[core], core))
+        lbs = [(S.hb, nhb), (S.hb, nhb)]
+    TPOFF = [0, 256, 0, 256]
+    anyd = any(DP)
+    last_k = len(CH) - 1
+    home = core if isr else owner[core]
+    peers = [c for c in cores if topo.chip(c) == topo.chip(core)]
+    me = peers.index(home) + (0 if isr else len(peers))
 
     def relay_for(src, dst):
         if topo.may_write(src, dst):
@@ -71,7 +97,6 @@ def rank_program(g, core, T, topo):
         halo.append((cores[r], cores[(r + 1) % n], "L", relay_for(cores[r], cores[(r + 1) % n])))
     jobs = [h for h in halo if h[3] is not None]
 
-    chips = sorted(set(topo.chip(c) for c in cores))
     plan = {}
     for ch in chips:
         mine = [c for c in cores if topo.chip(c) == ch]
@@ -83,8 +108,6 @@ def rank_program(g, core, T, topo):
             best = min(el, key=lambda c: (load[c], topo.die(c) != topo.die(d)))
             load[best] += 1
             plan.setdefault(best, []).append(d)
-    peers = [c for c in cores if topo.chip(c) == topo.chip(core)]
-    me = peers.index(core)
 
     def send(dst, out_ap, in_ap, rsem):
         rid, pid, _ = topo.addr(dst)
@@ -105,16 +128,19 @@ def rank_program(g, core, T, topo):
     def halo_ap(side):
         return (T.X[:, 1026:1028], S.hr) if side == "R" else (T.X[:, 0:2], S.hl)
 
-    SY.dma_start(T.EB[:, 0:2], T.u[:, 0:2]).then_inc(S.le, 16)
-    SY.dma_start(T.EB[:, 2:4], T.u[:, 1022:1024]).then_inc(S.le, 16)
-    for i, (a, b) in enumerate([(252, 516), (516, 772), (0, 252), (772, 1024)]):
-        SY.dma_start(T.X[:, a + 2:b + 2], T.u[:, a:b]).then_inc(S["lu%d" % i], 16)
+    if isr:
+        SY.dma_start(T.EB[:, 0:2], T.u[:, 0:2]).then_inc(S.le, 16)
+        SY.dma_start(T.EB[:, 2:4], T.u[:, 1022:1024]).then_inc(S.le, 16)
+        SY.dma_start(T.X[:, H0 - 2:H1 + 6], T.u[:, H0 - 4:H1 + 4]).then_inc(S.lu0, 16)
+        SY.dma_start(T.B[:, H0:H1], T.b[:, H0:H1]).then_inc(S.lbh, 16)
+        for i, (a, b) in enumerate([(124, 380), (644, 900), (0, 124), (900, 1024)]):
+            SY.dma_start(T.X[:, a + 2:b + 2], T.u[:, a:b]).then_inc(S["lu%d" % (i + 1)], 16)
 
     nms = 3
     V.memset(T.ZT[:, 0:1], 0.125).then_inc(S.ms, 1)
-    V.memset(T.ZT[:, 1:ZW + 1], 0.0).then_inc(S.ms, 1)
-    V.memset(T.ZT[:, ZW + 1:ZW + 2], 0.5).then_inc(S.ms, 1)
-    if ANYD:
+    V.memset(T.ZT[:, 1:129], 0.0).then_inc(S.ms, 1)
+    V.memset(T.ZT[:, 129:130], 0.5).then_inc(S.ms, 1)
+    if anyd:
         V.memset(T.ZN[:, 0:1], -1.0).then_inc(S.ms, 1)
         V.memset(T.ZN[:, 1:129], 0.0).then_inc(S.ms, 1)
         nms = 5
@@ -123,42 +149,48 @@ def rank_program(g, core, T, topo):
 
     SC.wait_ge(S.ms, nms)
     SC.dma_start(T.D8[:], T.ZT[:, 0:129]).then_inc(S.zd, 16)
-    SC.dma_start(T.D2[:], T.ZT[:, ZW - 127:ZW + 2]).then_inc(S.zd, 16)
+    SC.dma_start(T.D2[:], T.ZT[:, 1:130]).then_inc(S.zd, 16)
     nI = 2
-    if ANYD:
+    if anyd:
         SC.dma_start(T.DN[:], T.ZN[:, 0:129]).then_inc(S.zd, 16)
         nI = 3
-    SC.dma_start(T.B[:, 256:512], T.b[:, 256:512]).then_inc(S.lb0, 16)
-    SC.dma_start(T.B[:, 512:768], T.b[:, 512:768]).then_inc(S.lb1, 16)
+    if isr:
+        SC.dma_start(T.B[:, 128:384], T.b[:, 128:384]).then_inc(S.lb0, 16)
+        SC.dma_start(T.B[:, 640:896], T.b[:, 640:896]).then_inc(S.lb1, 16)
     SC.wait_ge(S.zd, 16 * nI)
     SC.dma_start(T.I8[:, :], T.D8[0:16384]).then_inc(S.li, 16)
     SC.dma_start(T.I2[:, :], T.D2[128:16512]).then_inc(S.li, 16)
-    if ANYD:
+    if anyd:
         SC.dma_start(T.IN[:, :], T.DN[0:16384]).then_inc(S.li, 16)
-    SC.dma_start(T.B[:, 0:256], T.b[:, 0:256]).then_inc(S.lb2, 16)
-    SC.dma_start(T.B[:, 768:1024], T.b[:, 768:1024]).then_inc(S.lb3, 16)
-    lbsem = [S.lb0, S.lb1, S.lb2, S.lb3, S.lb3]
+    if isr:
+        SC.dma_start(T.B[:, 0:128], T.b[:, 0:128]).then_inc(S.lb2, 16)
+        SC.dma_start(T.B[:, 896:1024], T.b[:, 896:1024]).then_inc(S.lb3, 16)
 
-    g.wait_ge(S.le, 32)
-    mysends = [h for h in halo if h[0] == core]
-    mysends.sort(key=lambda h: (h[3] is None, topo.chip(h[1]) == topo.chip(core)))
-    for h in mysends:
-        src_ap = T.EB[:, 0:2] if h[2] == "R" else T.EB[:, 2:4]
-        if h[3] is None:
-            ap, sem = halo_ap(h[2])
-            send(h[1], ap, src_ap, sem)
-        else:
-            j = jobs.index(h)
-            send(h[3], T.RB[:, 2 * j:2 * j + 2], src_ap, S["rl%d" % j])
-    for j, h in enumerate(jobs):
-        if h[3] == core:
-            g.wait_ge(S["rl%d" % j], pc(topo.mask(h[0], core)))
-            ap, sem = halo_ap(h[2])
-            send(h[1], ap, T.RB[:, 2 * j:2 * j + 2], sem)
     hcount = {}
-    for h in halo:
-        if h[1] == core:
-            hcount[h[2]] = pc(topo.mask(h[0] if h[3] is None else h[3], core))
+    if isr:
+        g.wait_ge(S.le, 32)
+        mysends = [h for h in halo if h[0] == core]
+        mysends.sort(key=lambda h: (h[3] is None, topo.chip(h[1]) == topo.chip(core)))
+        for h in mysends:
+            src_ap = T.EB[:, 0:2] if h[2] == "R" else T.EB[:, 2:4]
+            if h[3] is None:
+                ap, sem = halo_ap(h[2])
+                send(h[1], ap, src_ap, sem)
+            else:
+                j = jobs.index(h)
+                send(h[3], T.RB[:, 2 * j:2 * j + 2], src_ap, S["rl%d" % j])
+        g.wait_ge(S.lu0, 16)
+        send(helper[core], T.X[:, H0 - 2:H1 + 6], T.X[:, H0 - 2:H1 + 6], S.hx)
+        g.wait_ge(S.lbh, 16)
+        send(helper[core], T.B[:, H0:H1], T.B[:, H0:H1], S.hb)
+        for j, h in enumerate(jobs):
+            if h[3] == core:
+                g.wait_ge(S["rl%d" % j], pc(topo.mask(h[0], core)))
+                ap, sem = halo_ap(h[2])
+                send(h[1], ap, T.RB[:, 2 * j:2 * j + 2], sem)
+        for h in halo:
+            if h[1] == core:
+                hcount[h[2]] = pc(topo.mask(h[0] if h[3] is None else h[3], core))
 
     pev = {}
 
@@ -166,36 +198,50 @@ def rank_program(g, core, T, topo):
         pev[name] = ev()
         V.tensor_tensor(T.P[:, j0:j1], T.X[:, j0:j1], T.X[:, j0 + 1:j1 + 1], ADD).then_inc(pev[name], 1)
 
-    pdeps = [["A"], ["A", "B"], ["L", "C", "A"], ["B", "D"], ["D", "R"]]
     qev = {}
-    V.wait_ge(S.lu0, 16)
-    pairs("A", 254, 517)
-    if USEQ[0]:
-        c0, w = CHUNKS[0]
-        qev[0] = ev()
-        V.wait_ge(pev["A"], 1)
-        V.tensor_tensor(T.Q[:, c0:c0 + w], T.P[:, c0:c0 + w], T.P[:, c0 + 3:c0 + 3 + w], ADD).then_inc(qev[0], 1)
-    V.wait_ge(S.lu1, 16)
-    pairs("B", 517, 773)
-    V.wait_ge(S.lu2, 16)
-    pairs("C", 2, 254)
-    V.wait_ge(S.lu3, 16)
-    pairs("D", 773, 1025)
-    if ANYD:
+    if isr:
+        V.wait_ge(S.lu0, 16)
+        V.wait_ge(S.lu1, 16)
+        pairs("A", 126, 387)
+        if USEQ[0]:
+            c0, w = CH[0]
+            qev[0] = ev()
+            V.wait_ge(pev["A"], 1)
+            V.tensor_tensor(T.Q[:, c0:c0 + w], T.P[:, c0:c0 + w], T.P[:, c0 + 3:c0 + 3 + w], ADD).then_inc(qev[0], 1)
+        V.wait_ge(S.lu2, 16)
+        pairs("B", 640, 901)
+        V.wait_ge(S.lu3, 16)
+        pairs("C", 2, 126)
+        V.wait_ge(S.lu4, 16)
+        pairs("D", 901, 1025)
+    else:
+        V.wait_ge(S.hx, pc(topo.mask(owner[core], core)))
+        pairs("A", 384, 515)
+        pairs("B", 515, 643)
+    if anyd:
         V.wait_ge(S.ms, nms)
 
-    evY = [ev() for _ in CHUNKS]
+    evY = [ev() for _ in CH]
     eGS, eT, eTS, eO = ev(), ev(), ev(), ev()
+    yev = []
 
-    accS, accM = T.ACC[:, 0:256], T.ACC[:, 256:512]
+    def yout(k):
+        c0, w = CH[k]
+        e = ev()
+        yev.append((k, e))
+        if DP[k]:
+            V.tensor_tensor(T.Y[:, c0:c0 + w], T["Y%d" % k][:, 0:w], T.X[:, c0 + 2:c0 + 2 + w], ADD).then_inc(e, 1)
+        else:
+            V.tensor_copy(T.Y[:, c0:c0 + w], T["Y%d" % k][:, 0:w]).then_inc(e, 1)
+
     prev = None
-    for k, (c0, w) in enumerate(CHUNKS):
+    for k, (c0, w) in enumerate(CH):
         Yk = T["Y%d" % k][:, 0:w]
         Xc = T.X[:, c0 + 2:c0 + 2 + w]
         ds = T.DS[:, c0:c0 + w]
         V.wait_ge(evY[k], 1)
         e1 = ev()
-        if DPASS[k]:
+        if DP[k]:
             ps = Yk
             V.tensor_tensor(ds, T.ZT[:, 1:1 + w], Yk, SUB).then_inc(e1, 1)
             V.wait_ge(e1, 1)
@@ -207,6 +253,8 @@ def rank_program(g, core, T, topo):
         e2 = ev()
         if k == 0:
             os_, om = T.ACC[:, 0:w], T.ACC[:, 256:256 + w]
+        elif k == last_k and not isr:
+            os_, om = T.FS[:, :], T.FM[:, :]
         else:
             os_, om = T.NSQ[:, c0:c0 + w], T.AB[:, c0:c0 + w]
         V.tensor_tensor(os_, ps, ds, MUL).then_inc(e2, 1)
@@ -214,9 +262,12 @@ def rank_program(g, core, T, topo):
         V.wait_ge(e2, 2)
         if k == 0:
             prev = e2
-            V.wait_ge(S.hl, hcount["L"])
-            pairs("L", 0, 2)
-        elif k < 4:
+            if isr:
+                V.wait_ge(S.hl, hcount["L"])
+                pairs("L", 0, 2)
+            else:
+                yout(0)
+        elif k < last_k:
             V.wait_ge(prev, 2)
             e3 = ev()
             V.tensor_tensor(T.ACC[:, 0:w], T.ACC[:, 0:w], os_, ADD).then_inc(e3, 1)
@@ -225,7 +276,7 @@ def rank_program(g, core, T, topo):
             if k == 1:
                 V.wait_ge(S.hr, hcount["R"])
                 pairs("R", 1025, 1027)
-        else:
+        elif isr:
             V.wait_ge(prev, 2)
             e3 = ev()
             V.tensor_tensor(T.FS[:, :], T.ACC[:, 128:256], os_, ADD).then_inc(e3, 1)
@@ -260,7 +311,7 @@ def rank_program(g, core, T, topo):
     V.tensor_copy(T.L1[:, 4 * me:4 * me + 2], T.MP[:, 128:130]).then_inc(eMSG, 1)
 
     PE.wait_ge(S.li, 16 * nI)
-    for k, (c0, w) in enumerate(CHUNKS):
+    for k, (c0, w) in enumerate(CH):
         out = T["Y%d" % k][:, 0:w]
         taps = []
         if USEQ[k]:
@@ -271,11 +322,11 @@ def rank_program(g, core, T, topo):
                 PE.wait_ge(pev[nm], 1)
             taps.append((T.I8, T.P[:, c0:c0 + w]))
             taps.append((T.I8, T.P[:, c0 + 3:c0 + 3 + w]))
-        if DPASS[k]:
+        if DP[k]:
             taps.append((T.IN, T.X[:, c0 + 2:c0 + 2 + w]))
         for i, (m, r) in enumerate(taps):
             PE.matmul(out, m[:, :], r, i == 0, False)
-        PE.wait_ge(lbsem[k], 16)
+        PE.wait_ge(lbs[k][0], lbs[k][1])
         PE.matmul(out, T.I2[:, :], T.B[:, c0:c0 + w], False, True).then_inc(evY[k], 1)
     PE.wait_ge(eGS, 1)
     PE.matmul(T.MP[:, 0:128], T.GS[:, :], T.I8[:, :], True, True).then_inc(eT, 1)
@@ -283,29 +334,34 @@ def rank_program(g, core, T, topo):
     PE.wait_ge(eTS, 1)
     PE.matmul(T.MP[:, 128:130], T.TS[:, :], T.CV[:, :], True, True).then_inc(eO, 1)
 
+    if not isr:
+        c0, w = CH[0]
+        g.wait_ge(yev[0][1], 1)
+        send(home, T.Y[:, c0:c0 + w], T.Y[:, c0:c0 + w], S.yh)
+        g.wait_ge(eMSG, 2)
+        fused(peers, slot, [slot for _ in peers], S.a1)
+        yout(1)
+        c0, w = CH[1]
+        g.wait_ge(yev[1][1], 1)
+        send(home, T.Y[:, c0:c0 + w], T.Y[:, c0:c0 + w], S.yh)
+        g.wait_ge(S.ls, lsn[0])
+        return
+
     others = [c for c in peers if c != core]
     g.wait_ge(eMSG, 2)
     fused(others, slot, [slot for _ in others], S.a1)
-
-    yev = []
-
-    def yout(k):
-        c0, w = CHUNKS[k]
-        e = ev()
-        yev.append((k, e))
-        if DPASS[k]:
-            V.tensor_tensor(T.Y[:, c0:c0 + w], T["Y%d" % k][:, 0:w], T.X[:, c0 + 2:c0 + 2 + w], ADD).then_inc(e, 1)
-        else:
-            V.tensor_copy(T.Y[:, c0:c0 + w], T["Y%d" % k][:, 0:w]).then_inc(e, 1)
-
     for k in (0, 1, 2):
         yout(k)
     V.wait_ge(eMSG, 2)
-    V.wait_ge(S.a1, sum(pc(topo.mask(c, core)) for c in others))
+    V.wait_ge(S.a1, sum(pc(topo.mask(c, core)) for c in others) + sum(pc(topo.mask(helper[c], core)) for c in peers))
     e7 = ev()
-    V.tensor_tensor(T.A8[:, :], T.L1[:, 0:8], T.L1[:, 8:16], ADD).then_inc(e7, 1)
-    V.tensor_tensor(T.M8[:, :], T.L1[:, 0:8], T.L1[:, 8:16], MAX).then_inc(e7, 1)
+    V.tensor_tensor(T.A16[:, :], T.L1[:, 0:16], T.L1[:, 16:32], ADD).then_inc(e7, 1)
+    V.tensor_tensor(T.M16[:, :], T.L1[:, 0:16], T.L1[:, 16:32], MAX).then_inc(e7, 1)
     V.wait_ge(e7, 2)
+    e7b = ev()
+    V.tensor_tensor(T.A8[:, :], T.A16[:, 0:8], T.A16[:, 8:16], ADD).then_inc(e7b, 1)
+    V.tensor_tensor(T.M8[:, :], T.M16[:, 0:8], T.M16[:, 8:16], MAX).then_inc(e7b, 1)
+    V.wait_ge(e7b, 2)
     eC = ev()
     V.tensor_tensor(T.L2[:, 0:2], T.A8[:, 0:2], T.A8[:, 4:6], ADD).then_inc(eC, 1)
     V.tensor_tensor(T.L2[:, 2:4], T.M8[:, 2:4], T.M8[:, 6:8], MAX).then_inc(eC, 1)
@@ -320,8 +376,7 @@ def rank_program(g, core, T, topo):
         fused(plan[core], T.L2[:, 0:4], [slot2(topo.chip(core), d) for d in plan[core]], S.a2)
     g.wait_ge(S.ls, lsn[0])
 
-    for k in (3, 4):
-        yout(k)
+    yout(3)
     na2 = sum(pc(topo.mask(s, core)) for s in plan for d in plan[s] if d == core)
     V.wait_ge(eC, 2)
     V.wait_ge(S.a2, na2)
@@ -337,10 +392,12 @@ def rank_program(g, core, T, topo):
     V.tensor_tensor(T.WB[:, 2:3], T.M4B[:, 2:3], T.M4B[:, 3:4], MAX).then_inc(eS, 1)
 
     for k, e in yev:
-        c0, w = CHUNKS[k]
+        c0, w = CH[k]
         SC.wait_ge(e, 1)
         SC.dma_start(T.y[:, c0:c0 + w], T.Y[:, c0:c0 + w]).then_inc(S.ys, 16)
-    SC.wait_ge(S.ys, 16 * len(yev))
+    SC.wait_ge(S.yh, 2 * pc(topo.mask(helper[core], core)))
+    SC.dma_start(T.y[:, H0:H1], T.Y[:, H0:H1]).then_inc(S.ys, 16)
+    SC.wait_ge(S.ys, 16 * (len(yev) + 1))
     SY.wait_ge(eS, 1)
     SY.dma_start(T.s[:, :], T.WB[:, 1:3]).then_inc(S.ss, 16)
     SY.wait_ge(S.ss, 16)

@@ -1,36 +1,31 @@
+import math
 from concourse.bass import DstId, RemoteDMATransfer
-from concourse.mybir import AluOpType
+from concourse.mybir import AluOpType, AxisListType, ActivationFunctionType
 
 NR = 12
 WD = 1024
 H0, H1 = 384, 640
 NEV = 120
+PW = 264
 
 SCRATCH = {
     "X": ("sbuf", [128, 1028], "float32"), "B": ("sbuf", [128, 1024], "float32"),
-    "P": ("sbuf", [128, 1028], "float32"), "Q": ("sbuf", [128, 1024], "float32"),
+    "P": ("sbuf", [128, 4 * PW], "float32"), "Q": ("sbuf", [128, 1024], "float32"),
+    "R": ("sbuf", [128, 1024], "float32"), "D": ("sbuf", [128, 1024], "float32"),
+    "J": ("sbuf", [128, 1024], "float32"), "Y": ("sbuf", [128, 1024], "float32"),
     "EB": ("sbuf", [128, 4], "float32"), "RB": ("sbuf", [128, 8], "float32"),
-    "ZT": ("sbuf", [128, 130], "float32"), "ZN": ("sbuf", [128, 129], "float32"),
-    "I8": ("sbuf", [128, 128], "float32"), "I2": ("sbuf", [128, 128], "float32"), "IN": ("sbuf", [128, 128], "float32"),
-    "CV": ("sbuf", [128, 2], "float32"),
-    "DS": ("sbuf", [128, 1024], "float32"), "NSQ": ("sbuf", [128, 1024], "float32"),
-    "AB": ("sbuf", [128, 1024], "float32"), "Y": ("sbuf", [128, 1024], "float32"),
-    "FS": ("sbuf", [128, 128], "float32"), "FM": ("sbuf", [128, 128], "float32"),
-    "GS": ("sbuf", [128, 128], "float32"), "GM2": ("sbuf", [128, 64], "float32"),
-    "HM": ("sbuf", [128, 64], "float32"), "TR": ("sbuf", [128, 64], "float32"),
-    "TS": ("sbuf", [128, 128], "float32"),
+    "SS": ("sbuf", [128, 4], "float32"), "MX": ("sbuf", [128, 4], "float32"),
     "L1": ("sbuf", [128, 32], "float32"), "L2": ("sbuf", [128, 12], "float32"),
     "A16": ("sbuf", [128, 16], "float32"), "M16": ("sbuf", [128, 16], "float32"),
     "A8": ("sbuf", [128, 8], "float32"), "M8": ("sbuf", [128, 8], "float32"),
     "A4": ("sbuf", [128, 4], "float32"), "M4": ("sbuf", [128, 4], "float32"),
     "M4B": ("sbuf", [128, 4], "float32"), "WB": ("sbuf", [128, 4], "float32"),
-    "D8": ("dram", [16512], "float32"), "D2": ("dram", [16512], "float32"), "DN": ("dram", [16512], "float32"),
-    "Y0": ("psum", [128, 512], "float32"), "Y1": ("psum", [128, 512], "float32"),
-    "Y2": ("psum", [128, 512], "float32"), "Y3": ("psum", [128, 512], "float32"),
-    "TP": ("psum", [128, 512], "float32"),
-    "ACC": ("psum", [128, 512], "float32"), "MP": ("psum", [128, 512], "float32"),
+    "PA0": ("psum", [128, 512], "float32"), "PA1": ("psum", [128, 512], "float32"),
+    "PA2": ("psum", [128, 512], "float32"), "PA3": ("psum", [128, 512], "float32"),
+    "PB0": ("psum", [128, 512], "float32"), "PB1": ("psum", [128, 512], "float32"),
+    "PB2": ("psum", [128, 512], "float32"), "PB3": ("psum", [128, 512], "float32"),
 }
-SEMAPHORES = (["le", "ms", "ms2", "zd", "li", "hl", "hr", "a1", "a2", "ls", "ys", "ss", "hx", "hb", "yh", "lbh",
+SEMAPHORES = (["le", "hl", "hr", "a1", "a2", "ls", "ys", "ss", "hx", "hb", "yh", "lbh",
                "rl0", "rl1", "rl2", "rl3", "lu0", "lu1", "lu2", "lu3", "lu4", "lb0", "lb1", "lb2", "lb3"]
               + ["e%d" % i for i in range(NEV)])
 
@@ -51,8 +46,10 @@ def rank_program(g, core, T, topo):
     isr = core in helper
     if not isr and core not in owner:
         return
-    V, PE, SY, SC, S = g.vector, g.tensor, g.sync, g.scalar, T.sem
-    ADD, SUB, MUL, MAX = AluOpType.add, AluOpType.subtract, AluOpType.mult, AluOpType.max
+    V, SY, SC, S = g.vector, g.sync, g.scalar, T.sem
+    ADD, SUB, MAX = AluOpType.add, AluOpType.subtract, AluOpType.max
+    AX = AxisListType.X
+    COPY, SQUARE = ActivationFunctionType.Copy, ActivationFunctionType.Square
     nev = [0]
     lsn = [0]
 
@@ -64,22 +61,6 @@ def rank_program(g, core, T, topo):
     def pc(m):
         return bin(m).count("1")
 
-    if isr:
-        CH = [(128, 256), (640, 256), (0, 128), (896, 128)]
-        USEQ = [True, False, False, False]
-        DP = [False, False, False, False]
-        pdeps = [["A"], ["B"], ["L", "C", "A"], ["B", "D", "R"]]
-        lbs = [(S.lb0, 16), (S.lb1, 16), (S.lb2, 16), (S.lb3, 16)]
-    else:
-        CH = [(384, 128), (512, 128)]
-        USEQ = [False, False]
-        DP = [True, True]
-        pdeps = [["A"], ["A", "B"]]
-        nhb = pc(topo.mask(owner[core], core))
-        lbs = [(S.hb, nhb), (S.hb, nhb)]
-    TPOFF = [0, 256, 0, 256]
-    anyd = any(DP)
-    last_k = len(CH) - 1
     home = core if isr else owner[core]
     peers = [c for c in cores if topo.chip(c) == topo.chip(core)]
     me = peers.index(home) + (0 if isr else len(peers))
@@ -135,36 +116,12 @@ def rank_program(g, core, T, topo):
         SY.dma_start(T.B[:, H0:H1], T.b[:, H0:H1]).then_inc(S.lbh, 16)
         for i, (a, b) in enumerate([(124, 380), (644, 900), (0, 124), (900, 1024)]):
             SY.dma_start(T.X[:, a + 2:b + 2], T.u[:, a:b]).then_inc(S["lu%d" % (i + 1)], 16)
+        for i, (a, b) in enumerate([(128, 384), (640, 896), (0, 128), (896, 1024)]):
+            SC.dma_start(T.B[:, a:b], T.b[:, a:b]).then_inc(S["lb%d" % i], 16)
 
-    nms = 3
-    V.memset(T.ZT[:, 0:1], 0.125).then_inc(S.ms, 1)
-    V.memset(T.ZT[:, 1:129], 0.0).then_inc(S.ms, 1)
-    V.memset(T.ZT[:, 129:130], 0.5).then_inc(S.ms, 1)
-    if anyd:
-        V.memset(T.ZN[:, 0:1], -1.0).then_inc(S.ms, 1)
-        V.memset(T.ZN[:, 1:129], 0.0).then_inc(S.ms, 1)
-        nms = 5
-    V.memset(T.CV[:, 0:1], 0.0).then_inc(S.ms2, 1)
-    V.memset(T.CV[:, 1:2], -8.0 / (NR * WD)).then_inc(S.ms2, 1)
-
-    SC.wait_ge(S.ms, nms)
-    SC.dma_start(T.D8[:], T.ZT[:, 0:129]).then_inc(S.zd, 16)
-    SC.dma_start(T.D2[:], T.ZT[:, 1:130]).then_inc(S.zd, 16)
-    nI = 2
-    if anyd:
-        SC.dma_start(T.DN[:], T.ZN[:, 0:129]).then_inc(S.zd, 16)
-        nI = 3
-    if isr:
-        SC.dma_start(T.B[:, 128:384], T.b[:, 128:384]).then_inc(S.lb0, 16)
-        SC.dma_start(T.B[:, 640:896], T.b[:, 640:896]).then_inc(S.lb1, 16)
-    SC.wait_ge(S.zd, 16 * nI)
-    SC.dma_start(T.I8[:, :], T.D8[0:16384]).then_inc(S.li, 16)
-    SC.dma_start(T.I2[:, :], T.D2[128:16512]).then_inc(S.li, 16)
-    if anyd:
-        SC.dma_start(T.IN[:, :], T.DN[0:16384]).then_inc(S.li, 16)
-    if isr:
-        SC.dma_start(T.B[:, 0:128], T.b[:, 0:128]).then_inc(S.lb2, 16)
-        SC.dma_start(T.B[:, 896:1024], T.b[:, 896:1024]).then_inc(S.lb3, 16)
+    slot = T.L1[:, 4 * me:4 * me + 4]
+    eZ = ev()
+    V.memset(slot, 0.0).then_inc(eZ, 1)
 
     hcount = {}
     if isr:
@@ -192,166 +149,100 @@ def rank_program(g, core, T, topo):
             if h[1] == core:
                 hcount[h[2]] = pc(topo.mask(h[0] if h[3] is None else h[3], core))
 
-    pev = {}
-
-    def pairs(name, j0, j1):
-        pev[name] = ev()
-        V.tensor_tensor(T.P[:, j0:j1], T.X[:, j0:j1], T.X[:, j0 + 1:j1 + 1], ADD).then_inc(pev[name], 1)
-
-    qev = {}
     if isr:
-        V.wait_ge(S.lu0, 16)
-        V.wait_ge(S.lu1, 16)
-        pairs("A", 126, 387)
-        if USEQ[0]:
-            c0, w = CH[0]
-            qev[0] = ev()
-            V.wait_ge(pev["A"], 1)
-            V.tensor_tensor(T.Q[:, c0:c0 + w], T.P[:, c0:c0 + w], T.P[:, c0 + 3:c0 + 3 + w], ADD).then_inc(qev[0], 1)
-        V.wait_ge(S.lu2, 16)
-        pairs("B", 640, 901)
-        V.wait_ge(S.lu3, 16)
-        pairs("C", 2, 126)
-        V.wait_ge(S.lu4, 16)
-        pairs("D", 901, 1025)
+        CH = [(128, 256), (640, 256), (0, 128), (896, 128)]
+        uload = [[(S.lu0, 16), (S.lu1, 16)], [(S.lu0, 16), (S.lu2, 16)],
+                 [(S.lu1, 16), (S.lu3, 16), (S.hl, hcount["L"])], [(S.lu2, 16), (S.lu4, 16), (S.hr, hcount["R"])]]
+        bload = [(S.lb0, 16), (S.lb1, 16), (S.lb2, 16), (S.lb3, 16)]
+        VORD = [("p", 0), ("p", 1), ("q", 0), ("r", 0), ("q", 1), ("r", 1), ("d", 0), ("m", 0), ("p", 2), ("d", 1),
+                ("m", 1), ("p", 3), ("q", 2), ("r", 2), ("q", 3), ("r", 3), ("d", 2), ("m", 2), ("d", 3), ("m", 3)]
+        AORD = [("b4", 0), ("b4", 1), ("XP", 0), ("XP", 1), ("pP", 0), ("pP", 1), ("y", 0), ("y", 1), ("b4", 2),
+                ("XP", 2), ("sq", 0), ("b4", 3), ("XP", 3), ("sq", 1), ("pP", 2), ("pP", 3), ("y", 2), ("y", 3),
+                ("sq", 2), ("sq", 3)]
     else:
-        V.wait_ge(S.hx, pc(topo.mask(owner[core], core)))
-        pairs("A", 384, 515)
-        pairs("B", 515, 643)
-    if anyd:
-        V.wait_ge(S.ms, nms)
+        CH = [(384, 128), (512, 128)]
+        nh = pc(topo.mask(owner[core], core))
+        uload = [[(S.hx, nh)], [(S.hx, nh)]]
+        bload = [(S.hb, nh), (S.hb, nh)]
+        VORD = [("p", 0), ("p", 1), ("q", 0), ("r", 0), ("q", 1), ("r", 1), ("d", 0), ("m", 0), ("d", 1), ("m", 1)]
+        AORD = [("XP", 0), ("XP", 1), ("b4", 0), ("pP", 0), ("b4", 1), ("pP", 1), ("y", 0), ("y", 1), ("sq", 0),
+                ("sq", 1)]
+    nk = len(CH)
+    done = dict(((op, k), ev()) for k in range(nk) for op in ("b4", "XP", "p", "pP", "q", "r", "y", "d", "m", "sq"))
+    s0 = 1.0 / math.sqrt(float(NR * WD))
 
-    evY = [ev() for _ in CH]
-    eGS, eT, eTS, eO = ev(), ev(), ev(), ev()
-    yev = []
-
-    def yout(k):
+    for op, k in VORD:
         c0, w = CH[k]
-        e = ev()
-        yev.append((k, e))
-        if DP[k]:
-            V.tensor_tensor(T.Y[:, c0:c0 + w], T["Y%d" % k][:, 0:w], T.X[:, c0 + 2:c0 + 2 + w], ADD).then_inc(e, 1)
+        o = PW * k
+        PA, PB = T["PA%d" % k], T["PB%d" % k]
+        cs = slice(c0, c0 + w)
+        if op == "p":
+            for sm, cnt in uload[k]:
+                V.wait_ge(sm, cnt)
+            V.wait_ge(done[("XP", k)], 1)
+            ins = V.tensor_tensor(T.P[:, o:o + w + 3], T.X[:, c0:c0 + w + 3], PA[:, 0:w + 3], ADD)
+        elif op == "q":
+            V.wait_ge(done[("p", k)], 1)
+            V.wait_ge(done[("b4", k)], 1)
+            V.wait_ge(done[("pP", k)], 1)
+            ins = V.tensor_tensor(T.Q[:, cs], T.P[:, o:o + w], PB[:, 0:w], ADD)
+        elif op == "r":
+            V.wait_ge(done[("q", k)], 1)
+            ins = V.tensor_tensor(T.R[:, cs], T.Q[:, cs], PB[:, 256:256 + w], ADD)
+        elif op == "d":
+            V.wait_ge(done[("y", k)], 1)
+            ins = V.tensor_tensor(T.D[:, cs], T.Y[:, cs], PA[:, 1:w + 1], SUB)
         else:
-            V.tensor_copy(T.Y[:, c0:c0 + w], T["Y%d" % k][:, 0:w]).then_inc(e, 1)
+            V.wait_ge(done[("d", k)], 1)
+            ins = V.tensor_reduce(T.MX[:, k:k + 1], T.D[:, cs], AX, MAX, apply_absolute_value=True)
+        ins.then_inc(done[(op, k)], 1)
 
-    prev = None
-    for k, (c0, w) in enumerate(CH):
-        Yk = T["Y%d" % k][:, 0:w]
-        Xc = T.X[:, c0 + 2:c0 + 2 + w]
-        ds = T.DS[:, c0:c0 + w]
-        V.wait_ge(evY[k], 1)
-        e1 = ev()
-        if DP[k]:
-            ps = Yk
-            V.tensor_tensor(ds, T.ZT[:, 1:1 + w], Yk, SUB).then_inc(e1, 1)
-            V.wait_ge(e1, 1)
+    for op, k in AORD:
+        c0, w = CH[k]
+        o = PW * k
+        PA, PB = T["PA%d" % k], T["PB%d" % k]
+        cs = slice(c0, c0 + w)
+        if op == "b4":
+            SC.wait_ge(bload[k][0], bload[k][1])
+            ins = SC.activation(PB[:, 256:256 + w], T.B[:, cs], COPY, scale=4.0)
+        elif op == "XP":
+            for sm, cnt in uload[k]:
+                SC.wait_ge(sm, cnt)
+            ins = SC.activation(PA[:, 0:w + 3], T.X[:, c0 + 1:c0 + w + 4], COPY)
+        elif op == "pP":
+            SC.wait_ge(done[("p", k)], 1)
+            ins = SC.activation(PB[:, 0:w], T.P[:, o + 3:o + w + 3], COPY)
+        elif op == "y":
+            SC.wait_ge(done[("r", k)], 1)
+            ins = SC.activation(T.Y[:, cs], T.R[:, cs], COPY, scale=0.125)
         else:
-            ps = T.TP[:, TPOFF[k]:TPOFF[k] + w]
-            V.tensor_tensor(ds, Yk, Xc, SUB).then_inc(e1, 1)
-            V.tensor_tensor(ps, Xc, Yk, SUB).then_inc(e1, 1)
-            V.wait_ge(e1, 2)
-        e2 = ev()
-        if k == 0:
-            os_, om = T.ACC[:, 0:w], T.ACC[:, 256:256 + w]
-        elif k == last_k and not isr:
-            os_, om = T.FS[:, :], T.FM[:, :]
-        else:
-            os_, om = T.NSQ[:, c0:c0 + w], T.AB[:, c0:c0 + w]
-        V.tensor_tensor(os_, ps, ds, MUL).then_inc(e2, 1)
-        V.tensor_tensor(om, ps, ds, MAX).then_inc(e2, 1)
-        V.wait_ge(e2, 2)
-        if k == 0:
-            prev = e2
-            if isr:
-                V.wait_ge(S.hl, hcount["L"])
-                pairs("L", 0, 2)
-            else:
-                yout(0)
-        elif k < last_k:
-            V.wait_ge(prev, 2)
-            e3 = ev()
-            V.tensor_tensor(T.ACC[:, 0:w], T.ACC[:, 0:w], os_, ADD).then_inc(e3, 1)
-            V.tensor_tensor(T.ACC[:, 256:256 + w], T.ACC[:, 256:256 + w], om, MAX).then_inc(e3, 1)
-            prev = e3
-            if k == 1:
-                V.wait_ge(S.hr, hcount["R"])
-                pairs("R", 1025, 1027)
-        elif isr:
-            V.wait_ge(prev, 2)
-            e3 = ev()
-            V.tensor_tensor(T.FS[:, :], T.ACC[:, 128:256], os_, ADD).then_inc(e3, 1)
-            V.tensor_tensor(T.FM[:, :], T.ACC[:, 384:512], om, MAX).then_inc(e3, 1)
-            V.wait_ge(e3, 2)
-    V.tensor_tensor(T.GS[:, :], T.ACC[:, 0:128], T.FS[:, :], ADD).then_inc(eGS, 1)
-    e4 = ev()
-    V.tensor_tensor(T.TP[:, 384:448], T.ACC[:, 256:320], T.FM[:, 0:64], MAX).then_inc(e4, 1)
-    V.tensor_tensor(T.GM2[:, :], T.ACC[:, 320:384], T.FM[:, 64:128], MAX).then_inc(e4, 1)
-    V.wait_ge(e4, 2)
-    e5 = ev()
-    V.tensor_tensor(T.HM[:, :], T.TP[:, 384:448], T.GM2[:, :], MAX).then_inc(e5, 1)
-    V.wait_ge(e5, 1)
-    e6 = ev()
-    V.tensor_tensor(T.TR[:, 0:32], T.HM[:, 0:32], T.HM[:, 32:64], MAX).then_inc(e6, 1)
-    V.wait_ge(eT, 1)
-    V.tensor_copy(T.TS[:, :], T.MP[:, 0:128]).then_inc(eTS, 1)
-    slot = T.L1[:, 4 * me:4 * me + 4]
+            SC.wait_ge(done[("d", k)], 1)
+            ins = SC.activation(T.J[:, cs], T.D[:, cs], SQUARE, scale=s0, accum_out=T.SS[:, k:k + 1])
+        ins.then_inc(done[(op, k)], 1)
+
     eMSG = ev()
-    lo, wd, last = 0, 32, e6
-    while wd > 2:
-        h = wd // 2
-        V.wait_ge(last, 1)
-        if h == 2:
-            V.tensor_tensor(T.L1[:, 4 * me + 2:4 * me + 4], T.TR[:, lo:lo + h], T.TR[:, lo + h:lo + wd], MAX).then_inc(eMSG, 1)
-        else:
-            last = ev()
-            V.tensor_tensor(T.TR[:, lo + wd:lo + wd + h], T.TR[:, lo:lo + h], T.TR[:, lo + h:lo + wd], MAX).then_inc(last, 1)
-        lo += wd
-        wd = h
-    V.wait_ge(eO, 1)
-    V.tensor_copy(T.L1[:, 4 * me:4 * me + 2], T.MP[:, 128:130]).then_inc(eMSG, 1)
-
-    PE.wait_ge(S.li, 16 * nI)
-    for k, (c0, w) in enumerate(CH):
-        out = T["Y%d" % k][:, 0:w]
-        taps = []
-        if USEQ[k]:
-            PE.wait_ge(qev[k], 1)
-            taps.append((T.I8, T.Q[:, c0:c0 + w]))
-        else:
-            for nm in pdeps[k]:
-                PE.wait_ge(pev[nm], 1)
-            taps.append((T.I8, T.P[:, c0:c0 + w]))
-            taps.append((T.I8, T.P[:, c0 + 3:c0 + 3 + w]))
-        if DP[k]:
-            taps.append((T.IN, T.X[:, c0 + 2:c0 + 2 + w]))
-        for i, (m, r) in enumerate(taps):
-            PE.matmul(out, m[:, :], r, i == 0, False)
-        PE.wait_ge(lbs[k][0], lbs[k][1])
-        PE.matmul(out, T.I2[:, :], T.B[:, c0:c0 + w], False, True).then_inc(evY[k], 1)
-    PE.wait_ge(eGS, 1)
-    PE.matmul(T.MP[:, 0:128], T.GS[:, :], T.I8[:, :], True, True).then_inc(eT, 1)
-    PE.wait_ge(S.ms2, 2)
-    PE.wait_ge(eTS, 1)
-    PE.matmul(T.MP[:, 128:130], T.TS[:, :], T.CV[:, :], True, True).then_inc(eO, 1)
+    V.wait_ge(eZ, 1)
+    for k in range(nk):
+        V.wait_ge(done[("m", k)], 1)
+    V.tensor_reduce(T.L1[:, 4 * me + 2:4 * me + 3], T.MX[:, 0:nk], AX, MAX).then_inc(eMSG, 1)
+    for k in range(nk):
+        V.wait_ge(done[("sq", k)], 1)
+    V.tensor_reduce(T.L1[:, 4 * me + 1:4 * me + 2], T.SS[:, 0:nk], AX, ADD).then_inc(eMSG, 1)
 
     if not isr:
-        c0, w = CH[0]
-        g.wait_ge(yev[0][1], 1)
-        send(home, T.Y[:, c0:c0 + w], T.Y[:, c0:c0 + w], S.yh)
+        g.wait_ge(eZ, 1)
         g.wait_ge(eMSG, 2)
         fused(peers, slot, [slot for _ in peers], S.a1)
-        yout(1)
-        c0, w = CH[1]
-        g.wait_ge(yev[1][1], 1)
-        send(home, T.Y[:, c0:c0 + w], T.Y[:, c0:c0 + w], S.yh)
+        for k in range(nk):
+            g.wait_ge(done[("y", k)], 1)
+        send(home, T.Y[:, H0:H1], T.Y[:, H0:H1], S.yh)
         g.wait_ge(S.ls, lsn[0])
         return
 
     others = [c for c in peers if c != core]
+    g.wait_ge(eZ, 1)
     g.wait_ge(eMSG, 2)
     fused(others, slot, [slot for _ in others], S.a1)
-    for k in (0, 1, 2):
-        yout(k)
     V.wait_ge(eMSG, 2)
     V.wait_ge(S.a1, sum(pc(topo.mask(c, core)) for c in others) + sum(pc(topo.mask(helper[c], core)) for c in peers))
     e7 = ev()
@@ -376,7 +267,6 @@ def rank_program(g, core, T, topo):
         fused(plan[core], T.L2[:, 0:4], [slot2(topo.chip(core), d) for d in plan[core]], S.a2)
     g.wait_ge(S.ls, lsn[0])
 
-    yout(3)
     na2 = sum(pc(topo.mask(s, core)) for s in plan for d in plan[s] if d == core)
     V.wait_ge(eC, 2)
     V.wait_ge(S.a2, na2)
@@ -391,13 +281,12 @@ def rank_program(g, core, T, topo):
     eS = ev()
     V.tensor_tensor(T.WB[:, 2:3], T.M4B[:, 2:3], T.M4B[:, 3:4], MAX).then_inc(eS, 1)
 
-    for k, e in yev:
-        c0, w = CH[k]
-        SC.wait_ge(e, 1)
-        SC.dma_start(T.y[:, c0:c0 + w], T.Y[:, c0:c0 + w]).then_inc(S.ys, 16)
-    SC.wait_ge(S.yh, 2 * pc(topo.mask(helper[core], core)))
-    SC.dma_start(T.y[:, H0:H1], T.Y[:, H0:H1]).then_inc(S.ys, 16)
-    SC.wait_ge(S.ys, 16 * (len(yev) + 1))
-    SY.wait_ge(eS, 1)
-    SY.dma_start(T.s[:, :], T.WB[:, 1:3]).then_inc(S.ss, 16)
-    SY.wait_ge(S.ss, 16)
+    for k, (c0, w) in enumerate(CH):
+        SY.wait_ge(done[("y", k)], 1)
+        SY.dma_start(T.y[:, c0:c0 + w], T.Y[:, c0:c0 + w]).then_inc(S.ys, 16)
+    SY.wait_ge(S.yh, pc(topo.mask(helper[core], core)))
+    SY.dma_start(T.y[:, H0:H1], T.Y[:, H0:H1]).then_inc(S.ys, 16)
+    SY.wait_ge(S.ys, 16 * (nk + 1))
+    SC.wait_ge(eS, 1)
+    SC.dma_start(T.s[:, :], T.WB[:, 1:3]).then_inc(S.ss, 16)
+    SC.wait_ge(S.ss, 16)

@@ -4,48 +4,35 @@ from concourse.mybir import AluOpType, AxisListType, ActivationFunctionType
 
 NR = 12
 WD = 1024
-H0, H1 = 384, 640
 NEV = 120
 PW = 264
 
 SCRATCH = {
     "X": ("sbuf", [128, 1028], "float32"), "B": ("sbuf", [128, 1024], "float32"),
-    "P": ("sbuf", [128, 4 * PW], "float32"), "Q": ("sbuf", [128, 1024], "float32"),
+    "P": ("sbuf", [128, 5 * PW], "float32"), "Q": ("sbuf", [128, 1024], "float32"),
     "R": ("sbuf", [128, 1024], "float32"), "D": ("sbuf", [128, 1024], "float32"),
     "J": ("sbuf", [128, 1024], "float32"), "Y": ("sbuf", [128, 1024], "float32"),
     "EB": ("sbuf", [128, 4], "float32"), "RB": ("sbuf", [128, 8], "float32"),
-    "SS": ("sbuf", [128, 4], "float32"), "MX": ("sbuf", [128, 4], "float32"),
-    "L1": ("sbuf", [128, 32], "float32"), "L2": ("sbuf", [128, 12], "float32"),
-    "A16": ("sbuf", [128, 16], "float32"), "M16": ("sbuf", [128, 16], "float32"),
+    "SS": ("sbuf", [128, 8], "float32"), "MX": ("sbuf", [128, 8], "float32"),
+    "L1": ("sbuf", [128, 16], "float32"), "L2": ("sbuf", [128, 12], "float32"),
     "A8": ("sbuf", [128, 8], "float32"), "M8": ("sbuf", [128, 8], "float32"),
     "A4": ("sbuf", [128, 4], "float32"), "M4": ("sbuf", [128, 4], "float32"),
-    "M4B": ("sbuf", [128, 4], "float32"), "WB": ("sbuf", [128, 4], "float32"),
-    "PA0": ("psum", [128, 512], "float32"), "PA1": ("psum", [128, 512], "float32"),
-    "PA2": ("psum", [128, 512], "float32"), "PA3": ("psum", [128, 512], "float32"),
-    "PB0": ("psum", [128, 512], "float32"), "PB1": ("psum", [128, 512], "float32"),
-    "PB2": ("psum", [128, 512], "float32"), "PB3": ("psum", [128, 512], "float32"),
+    "WB": ("sbuf", [128, 4], "float32"),
+    "PS0": ("psum", [128, 512], "float32"), "PS1": ("psum", [128, 512], "float32"),
+    "PS2": ("psum", [128, 512], "float32"), "PS3": ("psum", [128, 512], "float32"),
+    "PS4": ("psum", [128, 512], "float32"), "PS5": ("psum", [128, 512], "float32"),
+    "PS6": ("psum", [128, 512], "float32"), "PS7": ("psum", [128, 512], "float32"),
 }
-SEMAPHORES = (["le", "hl", "hr", "a1", "a2", "ls", "ys", "ss", "hx", "hb", "yh", "lbh",
-               "rl0", "rl1", "rl2", "rl3", "lu0", "lu1", "lu2", "lu3", "lu4", "lb0", "lb1", "lb2", "lb3"]
-              + ["e%d" % i for i in range(NEV)])
+SEMAPHORES = (["le", "hl", "hr", "a1", "a2", "ls", "ys", "ss", "rl0", "rl1", "rl2", "rl3",
+               "lu0", "lu1", "lu2", "lb0", "lb1", "lb2"] + ["e%d" % i for i in range(NEV)])
 
 
 def rank_program(g, core, T, topo):
     cores = list(T.cores)
     n = len(cores)
-    chips = sorted(set(topo.chip(c) for c in cores))
-    helper = {}
-    for ch in chips:
-        mine = [c for c in cores if topo.chip(c) == ch]
-        idle = [c for c in range(max(0, min(mine) - 8), max(mine) + 8) if topo.chip(c) == ch and c not in cores]
-        for c in mine:
-            same = [i for i in idle if topo.die(i) == topo.die(c)]
-            helper[c] = (same or idle)[0]
-            idle.remove(helper[c])
-    owner = dict((h, c) for c, h in helper.items())
-    isr = core in helper
-    if not isr and core not in owner:
+    if core not in cores:
         return
+    chips = sorted(set(topo.chip(c) for c in cores))
     V, SY, SC, S = g.vector, g.sync, g.scalar, T.sem
     ADD, SUB, MAX = AluOpType.add, AluOpType.subtract, AluOpType.max
     AX = AxisListType.X
@@ -61,9 +48,8 @@ def rank_program(g, core, T, topo):
     def pc(m):
         return bin(m).count("1")
 
-    home = core if isr else owner[core]
     peers = [c for c in cores if topo.chip(c) == topo.chip(core)]
-    me = peers.index(home) + (0 if isr else len(peers))
+    me = peers.index(core)
 
     def relay_for(src, dst):
         if topo.may_write(src, dst):
@@ -109,109 +95,98 @@ def rank_program(g, core, T, topo):
     def halo_ap(side):
         return (T.X[:, 1026:1028], S.hr) if side == "R" else (T.X[:, 0:2], S.hl)
 
-    if isr:
-        SY.dma_start(T.EB[:, 0:2], T.u[:, 0:2]).then_inc(S.le, 16)
-        SY.dma_start(T.EB[:, 2:4], T.u[:, 1022:1024]).then_inc(S.le, 16)
-        SY.dma_start(T.X[:, H0 - 2:H1 + 6], T.u[:, H0 - 4:H1 + 4]).then_inc(S.lu0, 16)
-        SY.dma_start(T.B[:, H0:H1], T.b[:, H0:H1]).then_inc(S.lbh, 16)
-        for i, (a, b) in enumerate([(124, 380), (644, 900), (0, 124), (900, 1024)]):
-            SY.dma_start(T.X[:, a + 2:b + 2], T.u[:, a:b]).then_inc(S["lu%d" % (i + 1)], 16)
-        for i, (a, b) in enumerate([(128, 384), (640, 896), (0, 128), (896, 1024)]):
-            SC.dma_start(T.B[:, a:b], T.b[:, a:b]).then_inc(S["lb%d" % i], 16)
+    SY.dma_start(T.EB[:, 0:2], T.u[:, 0:2]).then_inc(S.le, 16)
+    SY.dma_start(T.EB[:, 2:4], T.u[:, 1022:1024]).then_inc(S.le, 16)
+    for i, (a, b) in enumerate([(0, 388), (388, 644), (644, 1024)]):
+        SY.dma_start(T.X[:, a + 2:b + 2], T.u[:, a:b]).then_inc(S["lu%d" % i], 16)
+    for i, (a, b) in enumerate([(0, 384), (384, 640), (640, 1024)]):
+        SC.dma_start(T.B[:, a:b], T.b[:, a:b]).then_inc(S["lb%d" % i], 16)
 
     slot = T.L1[:, 4 * me:4 * me + 4]
     eZ = ev()
     V.memset(slot, 0.0).then_inc(eZ, 1)
 
     hcount = {}
-    if isr:
-        g.wait_ge(S.le, 32)
-        mysends = [h for h in halo if h[0] == core]
-        mysends.sort(key=lambda h: (h[3] is None, topo.chip(h[1]) == topo.chip(core)))
-        for h in mysends:
-            src_ap = T.EB[:, 0:2] if h[2] == "R" else T.EB[:, 2:4]
-            if h[3] is None:
-                ap, sem = halo_ap(h[2])
-                send(h[1], ap, src_ap, sem)
-            else:
-                j = jobs.index(h)
-                send(h[3], T.RB[:, 2 * j:2 * j + 2], src_ap, S["rl%d" % j])
-        g.wait_ge(S.lu0, 16)
-        send(helper[core], T.X[:, H0 - 2:H1 + 6], T.X[:, H0 - 2:H1 + 6], S.hx)
-        g.wait_ge(S.lbh, 16)
-        send(helper[core], T.B[:, H0:H1], T.B[:, H0:H1], S.hb)
-        for j, h in enumerate(jobs):
-            if h[3] == core:
-                g.wait_ge(S["rl%d" % j], pc(topo.mask(h[0], core)))
-                ap, sem = halo_ap(h[2])
-                send(h[1], ap, T.RB[:, 2 * j:2 * j + 2], sem)
-        for h in halo:
-            if h[1] == core:
-                hcount[h[2]] = pc(topo.mask(h[0] if h[3] is None else h[3], core))
+    g.wait_ge(S.le, 32)
+    mysends = [h for h in halo if h[0] == core]
+    mysends.sort(key=lambda h: (h[3] is None, topo.chip(h[1]) == topo.chip(core)))
+    for h in mysends:
+        src_ap = T.EB[:, 0:2] if h[2] == "R" else T.EB[:, 2:4]
+        if h[3] is None:
+            ap, sem = halo_ap(h[2])
+            send(h[1], ap, src_ap, sem)
+        else:
+            j = jobs.index(h)
+            send(h[3], T.RB[:, 2 * j:2 * j + 2], src_ap, S["rl%d" % j])
+    for j, h in enumerate(jobs):
+        if h[3] == core:
+            g.wait_ge(S["rl%d" % j], pc(topo.mask(h[0], core)))
+            ap, sem = halo_ap(h[2])
+            send(h[1], ap, T.RB[:, 2 * j:2 * j + 2], sem)
+    for h in halo:
+        if h[1] == core:
+            hcount[h[2]] = pc(topo.mask(h[0] if h[3] is None else h[3], core))
 
-    if isr:
-        CH = [(128, 256), (640, 256), (0, 128), (896, 128)]
-        uload = [[(S.lu0, 16), (S.lu1, 16)], [(S.lu0, 16), (S.lu2, 16)],
-                 [(S.lu1, 16), (S.lu3, 16), (S.hl, hcount["L"])], [(S.lu2, 16), (S.lu4, 16), (S.hr, hcount["R"])]]
-        bload = [(S.lb0, 16), (S.lb1, 16), (S.lb2, 16), (S.lb3, 16)]
-        VORD = [("p", 0), ("p", 1), ("q", 0), ("r", 0), ("q", 1), ("r", 1), ("d", 0), ("m", 0), ("p", 2), ("d", 1),
-                ("m", 1), ("p", 3), ("q", 2), ("r", 2), ("q", 3), ("r", 3), ("d", 2), ("m", 2), ("d", 3), ("m", 3)]
-        AORD = [("b4", 0), ("b4", 1), ("XP", 0), ("XP", 1), ("pP", 0), ("pP", 1), ("y", 0), ("y", 1), ("b4", 2),
-                ("XP", 2), ("sq", 0), ("b4", 3), ("XP", 3), ("sq", 1), ("pP", 2), ("pP", 3), ("y", 2), ("y", 3),
-                ("sq", 2), ("sq", 3)]
-    else:
-        CH = [(384, 128), (512, 128)]
-        nh = pc(topo.mask(owner[core], core))
-        uload = [[(S.hx, nh)], [(S.hx, nh)]]
-        bload = [(S.hb, nh), (S.hb, nh)]
-        VORD = [("p", 0), ("p", 1), ("q", 0), ("r", 0), ("q", 1), ("r", 1), ("d", 0), ("m", 0), ("d", 1), ("m", 1)]
-        AORD = [("XP", 0), ("XP", 1), ("b4", 0), ("pP", 0), ("b4", 1), ("pP", 1), ("y", 0), ("y", 1), ("sq", 0),
-                ("sq", 1)]
+    CH = [(128, 256), (384, 256), (640, 256), (0, 128), (896, 128)]
+    PL = [((0, 0), (1, 0), (1, 256)), ((2, 0), (3, 0), (3, 256)), ((4, 0), (5, 0), (5, 256)),
+          ((6, 0), (6, 132), (6, 260)), ((7, 0), (7, 132), (7, 260))]
+    uload = [[(S.lu0, 16)], [(S.lu0, 16), (S.lu1, 16)], [(S.lu1, 16), (S.lu2, 16)],
+             [(S.lu0, 16), (S.hl, hcount["L"])], [(S.lu2, 16), (S.hr, hcount["R"])]]
+    bload = [(S.lb0, 16), (S.lb1, 16), (S.lb2, 16), (S.lb0, 16), (S.lb2, 16)]
+    VORD = "p0 p1 q0 r0 q1 p2 d0 r1 q2 m0 d1 r2 p3 p4 m1 d2 q3 q4 r3 r4 m2 d3 d4 m3 m4".split()
+    AORD = ("XP0 b40 b43 XP1 b41 pP0 b42 pP1 XP2 y0 b44 pP2 sq0 y1 XP3 XP4 sq1 y2 pP3 pP4 sq2 y3 y4 sq3 "
+            "sq4").split()
     nk = len(CH)
     done = dict(((op, k), ev()) for k in range(nk) for op in ("b4", "XP", "p", "pP", "q", "r", "y", "d", "m", "sq"))
     s0 = 1.0 / math.sqrt(float(NR * WD))
 
-    for op, k in VORD:
+    def place(k, i, a, b):
+        bank, off = PL[k][i]
+        return T["PS%d" % bank][:, off + a:off + b]
+
+    for name in VORD:
+        op, k = name[:-1], int(name[-1])
         c0, w = CH[k]
         o = PW * k
-        PA, PB = T["PA%d" % k], T["PB%d" % k]
         cs = slice(c0, c0 + w)
         if op == "p":
             for sm, cnt in uload[k]:
                 V.wait_ge(sm, cnt)
             V.wait_ge(done[("XP", k)], 1)
-            ins = V.tensor_tensor(T.P[:, o:o + w + 3], T.X[:, c0:c0 + w + 3], PA[:, 0:w + 3], ADD)
+            if PL[k][2][0] == PL[k][0][0]:
+                V.wait_ge(done[("b4", k)], 1)
+            ins = V.tensor_tensor(T.P[:, o:o + w + 3], T.X[:, c0:c0 + w + 3], place(k, 0, 0, w + 3), ADD)
         elif op == "q":
             V.wait_ge(done[("p", k)], 1)
             V.wait_ge(done[("b4", k)], 1)
             V.wait_ge(done[("pP", k)], 1)
-            ins = V.tensor_tensor(T.Q[:, cs], T.P[:, o:o + w], PB[:, 0:w], ADD)
+            ins = V.tensor_tensor(T.Q[:, cs], T.P[:, o:o + w], place(k, 1, 0, w), ADD)
         elif op == "r":
             V.wait_ge(done[("q", k)], 1)
-            ins = V.tensor_tensor(T.R[:, cs], T.Q[:, cs], PB[:, 256:256 + w], ADD)
+            ins = V.tensor_tensor(T.R[:, cs], T.Q[:, cs], place(k, 2, 0, w), ADD)
         elif op == "d":
             V.wait_ge(done[("y", k)], 1)
-            ins = V.tensor_tensor(T.D[:, cs], T.Y[:, cs], PA[:, 1:w + 1], SUB)
+            ins = V.tensor_tensor(T.D[:, cs], T.Y[:, cs], place(k, 0, 1, w + 1), SUB)
         else:
             V.wait_ge(done[("d", k)], 1)
             ins = V.tensor_reduce(T.MX[:, k:k + 1], T.D[:, cs], AX, MAX, apply_absolute_value=True)
         ins.then_inc(done[(op, k)], 1)
 
-    for op, k in AORD:
+    for name in AORD:
+        op, k = name[:-1], int(name[-1])
         c0, w = CH[k]
         o = PW * k
-        PA, PB = T["PA%d" % k], T["PB%d" % k]
         cs = slice(c0, c0 + w)
         if op == "b4":
             SC.wait_ge(bload[k][0], bload[k][1])
-            ins = SC.activation(PB[:, 256:256 + w], T.B[:, cs], COPY, scale=4.0)
+            ins = SC.activation(place(k, 2, 0, w), T.B[:, cs], COPY, scale=4.0)
         elif op == "XP":
             for sm, cnt in uload[k]:
                 SC.wait_ge(sm, cnt)
-            ins = SC.activation(PA[:, 0:w + 3], T.X[:, c0 + 1:c0 + w + 4], COPY)
+            ins = SC.activation(place(k, 0, 0, w + 3), T.X[:, c0 + 1:c0 + w + 4], COPY)
         elif op == "pP":
             SC.wait_ge(done[("p", k)], 1)
-            ins = SC.activation(PB[:, 0:w], T.P[:, o + 3:o + w + 3], COPY)
+            ins = SC.activation(place(k, 1, 0, w), T.P[:, o + 3:o + w + 3], COPY)
         elif op == "y":
             SC.wait_ge(done[("r", k)], 1)
             ins = SC.activation(T.Y[:, cs], T.R[:, cs], COPY, scale=0.125)
@@ -229,29 +204,20 @@ def rank_program(g, core, T, topo):
         V.wait_ge(done[("sq", k)], 1)
     V.tensor_reduce(T.L1[:, 4 * me + 1:4 * me + 2], T.SS[:, 0:nk], AX, ADD).then_inc(eMSG, 1)
 
-    if not isr:
-        g.wait_ge(eZ, 1)
-        g.wait_ge(eMSG, 2)
-        fused(peers, slot, [slot for _ in peers], S.a1)
-        for k in range(nk):
-            g.wait_ge(done[("y", k)], 1)
-        send(home, T.Y[:, H0:H1], T.Y[:, H0:H1], S.yh)
-        g.wait_ge(S.ls, lsn[0])
-        return
-
     others = [c for c in peers if c != core]
+    most = max(len(plan.get(c, [])) for c in peers)
+    first = [c for c in others if len(plan.get(c, [])) == most]
+    rest = [c for c in others if c not in first]
     g.wait_ge(eZ, 1)
     g.wait_ge(eMSG, 2)
-    fused(others, slot, [slot for _ in others], S.a1)
+    for grp in (first, rest):
+        if grp:
+            fused(grp, slot, [slot for _ in grp], S.a1)
     V.wait_ge(eMSG, 2)
-    V.wait_ge(S.a1, sum(pc(topo.mask(c, core)) for c in others) + sum(pc(topo.mask(helper[c], core)) for c in peers))
-    e7 = ev()
-    V.tensor_tensor(T.A16[:, :], T.L1[:, 0:16], T.L1[:, 16:32], ADD).then_inc(e7, 1)
-    V.tensor_tensor(T.M16[:, :], T.L1[:, 0:16], T.L1[:, 16:32], MAX).then_inc(e7, 1)
-    V.wait_ge(e7, 2)
+    V.wait_ge(S.a1, sum(pc(topo.mask(c, core)) for c in others))
     e7b = ev()
-    V.tensor_tensor(T.A8[:, :], T.A16[:, 0:8], T.A16[:, 8:16], ADD).then_inc(e7b, 1)
-    V.tensor_tensor(T.M8[:, :], T.M16[:, 0:8], T.M16[:, 8:16], MAX).then_inc(e7b, 1)
+    V.tensor_tensor(T.A8[:, :], T.L1[:, 0:8], T.L1[:, 8:16], ADD).then_inc(e7b, 1)
+    V.tensor_tensor(T.M8[:, :], T.L1[:, 0:8], T.L1[:, 8:16], MAX).then_inc(e7b, 1)
     V.wait_ge(e7b, 2)
     eC = ev()
     V.tensor_tensor(T.L2[:, 0:2], T.A8[:, 0:2], T.A8[:, 4:6], ADD).then_inc(eC, 1)
@@ -274,19 +240,16 @@ def rank_program(g, core, T, topo):
     V.tensor_tensor(T.A4[:, :], T.L2[:, 0:4], T.L2[:, 4:8], ADD).then_inc(e8, 1)
     V.tensor_tensor(T.M4[:, :], T.L2[:, 0:4], T.L2[:, 4:8], MAX).then_inc(e8, 1)
     V.wait_ge(e8, 2)
-    e9 = ev()
-    V.tensor_tensor(T.WB[:, :], T.A4[:, :], T.L2[:, 8:12], ADD).then_inc(e9, 1)
-    V.tensor_tensor(T.M4B[:, :], T.M4[:, :], T.L2[:, 8:12], MAX).then_inc(e9, 1)
-    V.wait_ge(e9, 2)
     eS = ev()
-    V.tensor_tensor(T.WB[:, 2:3], T.M4B[:, 2:3], T.M4B[:, 3:4], MAX).then_inc(eS, 1)
+    V.tensor_tensor(T.WB[:, 1:2], T.A4[:, 1:2], T.L2[:, 9:10], ADD).then_inc(eS, 1)
+    V.tensor_tensor(T.WB[:, 2:3], T.M4[:, 2:3], T.L2[:, 10:11], MAX).then_inc(eS, 1)
 
-    for k, (c0, w) in enumerate(CH):
-        SY.wait_ge(done[("y", k)], 1)
-        SY.dma_start(T.y[:, c0:c0 + w], T.Y[:, c0:c0 + w]).then_inc(S.ys, 16)
-    SY.wait_ge(S.yh, pc(topo.mask(helper[core], core)))
-    SY.dma_start(T.y[:, H0:H1], T.Y[:, H0:H1]).then_inc(S.ys, 16)
-    SY.wait_ge(S.ys, 16 * (nk + 1))
-    SC.wait_ge(eS, 1)
+    stores = [((0, 1), 128, 640), ((2,), 640, 896), ((3,), 0, 128), ((4,), 896, 1024)]
+    for ks, a, b in stores:
+        for k in ks:
+            SY.wait_ge(done[("y", k)], 1)
+        SY.dma_start(T.y[:, a:b], T.Y[:, a:b]).then_inc(S.ys, 16)
+    SY.wait_ge(S.ys, 16 * len(stores))
+    SC.wait_ge(eS, 2)
     SC.dma_start(T.s[:, :], T.WB[:, 1:3]).then_inc(S.ss, 16)
     SC.wait_ge(S.ss, 16)

@@ -15,15 +15,13 @@ SCRATCH = {
     "EB": ("sbuf", [128, 4], "float32"), "RB": ("sbuf", [128, 8], "float32"),
     "SS": ("sbuf", [128, 8], "float32"), "MX": ("sbuf", [128, 8], "float32"),
     "L1": ("sbuf", [128, 16], "float32"), "L2": ("sbuf", [128, 12], "float32"),
-    "A8": ("sbuf", [128, 8], "float32"), "M8": ("sbuf", [128, 8], "float32"),
-    "A4": ("sbuf", [128, 4], "float32"), "M4": ("sbuf", [128, 4], "float32"),
     "WB": ("sbuf", [128, 4], "float32"),
     "PS0": ("psum", [128, 512], "float32"), "PS1": ("psum", [128, 512], "float32"),
     "PS2": ("psum", [128, 512], "float32"), "PS3": ("psum", [128, 512], "float32"),
     "PS4": ("psum", [128, 512], "float32"), "PS5": ("psum", [128, 512], "float32"),
     "PS6": ("psum", [128, 512], "float32"), "PS7": ("psum", [128, 512], "float32"),
 }
-SEMAPHORES = (["le", "hl", "hr", "a1", "a2", "ls", "ys", "ss", "rl0", "rl1", "rl2", "rl3",
+SEMAPHORES = (["le", "hl", "hr", "a1", "a2", "ls", "l1", "ys", "ss", "rl0", "rl1", "rl2", "rl3",
                "lu0", "lu1", "lu2", "lb0", "lb1", "lb2"] + ["e%d" % i for i in range(NEV)])
 
 
@@ -39,6 +37,7 @@ def rank_program(g, core, T, topo):
     COPY, SQUARE = ActivationFunctionType.Copy, ActivationFunctionType.Square
     nev = [0]
     lsn = [0]
+    l1n = [0]
 
     def ev():
         s = S["e%d" % nev[0]]
@@ -83,20 +82,19 @@ def rank_program(g, core, T, topo):
                      dma_engine_mask=m)
         lsn[0] += pc(m)
 
-    def fused(dsts, src, dst_aps, rsem):
+    def fused(dsts, src, dst_aps, rsem, step1=False):
         m = topo.mask(core, dsts[0])
         for d in dsts:
             m &= topo.mask(core, d)
         ids = [DstId(rid=topo.addr(d)[0], pnc=topo.addr(d)[1]) for d in dsts]
         g.remote_dma_fused([RemoteDMATransfer(dst_ids=ids, dma_engine_mask=m, remote_sem=rsem, srcs=[src],
-                                              dsts=dst_aps, alu_op=0)], local_sem=S.ls)
-        lsn[0] += pc(m)
+                                              dsts=dst_aps, alu_op=0)], local_sem=S.l1 if step1 else S.ls)
+        (l1n if step1 else lsn)[0] += pc(m)
 
     def halo_ap(side):
         return (T.X[:, 1026:1028], S.hr) if side == "R" else (T.X[:, 0:2], S.hl)
 
-    SY.dma_start(T.EB[:, 0:2], T.u[:, 0:2]).then_inc(S.le, 16)
-    SY.dma_start(T.EB[:, 2:4], T.u[:, 1022:1024]).then_inc(S.le, 16)
+    SY.dma_start(T.EB[:, 0:2], T.u[:, 1022:1024]).then_inc(S.le, 16)
     for i, (a, b) in enumerate([(0, 388), (388, 644), (644, 1024)]):
         SY.dma_start(T.X[:, a + 2:b + 2], T.u[:, a:b]).then_inc(S["lu%d" % i], 16)
     for i, (a, b) in enumerate([(0, 384), (384, 640), (640, 1024)]):
@@ -105,13 +103,18 @@ def rank_program(g, core, T, topo):
     slot = T.L1[:, 4 * me:4 * me + 4]
     eZ = ev()
     V.memset(slot, 0.0).then_inc(eZ, 1)
+    V.memset(T.L2[:, 0:4], 0.0).then_inc(eZ, 1)
 
     hcount = {}
-    g.wait_ge(S.le, 32)
     mysends = [h for h in halo if h[0] == core]
-    mysends.sort(key=lambda h: (h[3] is None, topo.chip(h[1]) == topo.chip(core)))
+    mysends.sort(key=lambda h: h[2] == "R")
     for h in mysends:
-        src_ap = T.EB[:, 0:2] if h[2] == "R" else T.EB[:, 2:4]
+        if h[2] == "R":
+            g.wait_ge(S.lu0, 16)
+            src_ap = T.X[:, 2:4]
+        else:
+            g.wait_ge(S.le, 16)
+            src_ap = T.EB[:, 0:2]
         if h[3] is None:
             ap, sem = halo_ap(h[2])
             send(h[1], ap, src_ap, sem)
@@ -196,7 +199,7 @@ def rank_program(g, core, T, topo):
         ins.then_inc(done[(op, k)], 1)
 
     eMSG = ev()
-    V.wait_ge(eZ, 1)
+    V.wait_ge(eZ, 2)
     for k in range(nk):
         V.wait_ge(done[("m", k)], 1)
     V.tensor_reduce(T.L1[:, 4 * me + 2:4 * me + 3], T.MX[:, 0:nk], AX, MAX).then_inc(eMSG, 1)
@@ -208,20 +211,16 @@ def rank_program(g, core, T, topo):
     most = max(len(plan.get(c, [])) for c in peers)
     first = [c for c in others if len(plan.get(c, [])) == most]
     rest = [c for c in others if c not in first]
-    g.wait_ge(eZ, 1)
+    g.wait_ge(eZ, 2)
     g.wait_ge(eMSG, 2)
     for grp in (first, rest):
         if grp:
-            fused(grp, slot, [slot for _ in grp], S.a1)
+            fused(grp, slot, [slot for _ in grp], S.a1, True)
     V.wait_ge(eMSG, 2)
     V.wait_ge(S.a1, sum(pc(topo.mask(c, core)) for c in others))
-    e7b = ev()
-    V.tensor_tensor(T.A8[:, :], T.L1[:, 0:8], T.L1[:, 8:16], ADD).then_inc(e7b, 1)
-    V.tensor_tensor(T.M8[:, :], T.L1[:, 0:8], T.L1[:, 8:16], MAX).then_inc(e7b, 1)
-    V.wait_ge(e7b, 2)
     eC = ev()
-    V.tensor_tensor(T.L2[:, 0:2], T.A8[:, 0:2], T.A8[:, 4:6], ADD).then_inc(eC, 1)
-    V.tensor_tensor(T.L2[:, 2:4], T.M8[:, 2:4], T.M8[:, 6:8], MAX).then_inc(eC, 1)
+    V.tensor_reduce(T.L2[:, 1:2], T.L1[:, 1:16:4], AX, ADD).then_inc(eC, 1)
+    V.tensor_reduce(T.L2[:, 2:3], T.L1[:, 2:16:4], AX, MAX).then_inc(eC, 1)
 
     def slot2(src_chip, dst):
         oth = [x for x in chips if x != topo.chip(dst)]
@@ -232,22 +231,21 @@ def rank_program(g, core, T, topo):
         g.wait_ge(eC, 2)
         fused(plan[core], T.L2[:, 0:4], [slot2(topo.chip(core), d) for d in plan[core]], S.a2)
     g.wait_ge(S.ls, lsn[0])
+    g.wait_ge(S.l1, l1n[0])
 
     na2 = sum(pc(topo.mask(s, core)) for s in plan for d in plan[s] if d == core)
     V.wait_ge(eC, 2)
     V.wait_ge(S.a2, na2)
-    e8 = ev()
-    V.tensor_tensor(T.A4[:, :], T.L2[:, 0:4], T.L2[:, 4:8], ADD).then_inc(e8, 1)
-    V.tensor_tensor(T.M4[:, :], T.L2[:, 0:4], T.L2[:, 4:8], MAX).then_inc(e8, 1)
-    V.wait_ge(e8, 2)
     eS = ev()
-    V.tensor_tensor(T.WB[:, 1:2], T.A4[:, 1:2], T.L2[:, 9:10], ADD).then_inc(eS, 1)
-    V.tensor_tensor(T.WB[:, 2:3], T.M4[:, 2:3], T.L2[:, 10:11], MAX).then_inc(eS, 1)
+    V.tensor_reduce(T.WB[:, 1:2], T.L2[:, 1:12:4], AX, ADD).then_inc(eS, 1)
+    V.tensor_reduce(T.WB[:, 2:3], T.L2[:, 2:12:4], AX, MAX).then_inc(eS, 1)
 
     stores = [((0, 1), 128, 640), ((2,), 640, 896), ((3,), 0, 128), ((4,), 896, 1024)]
-    for ks, a, b in stores:
+    for i, (ks, a, b) in enumerate(stores):
         for k in ks:
             SY.wait_ge(done[("y", k)], 1)
+        if i == 2:
+            SY.wait_ge(S.l1, l1n[0])
         SY.dma_start(T.y[:, a:b], T.Y[:, a:b]).then_inc(S.ys, 16)
     SY.wait_ge(S.ys, 16 * len(stores))
     SC.wait_ge(eS, 2)

@@ -5,23 +5,21 @@ from concourse.mybir import AluOpType, AxisListType, ActivationFunctionType
 NR = 12
 WD = 1024
 NEV = 120
-PW = 264
 
 SCRATCH = {
     "X": ("sbuf", [128, 1028], "float32"), "B": ("sbuf", [128, 1024], "float32"),
-    "P": ("sbuf", [128, 5 * PW], "float32"), "Q": ("sbuf", [128, 1024], "float32"),
-    "R": ("sbuf", [128, 1024], "float32"), "D": ("sbuf", [128, 1024], "float32"),
-    "J": ("sbuf", [128, 1024], "float32"), "Y": ("sbuf", [128, 1024], "float32"),
+    "W5": ("sbuf", [128, 1024], "float32"), "E": ("sbuf", [128, 1024], "float32"),
+    "D8": ("sbuf", [128, 1024], "float32"), "D": ("sbuf", [128, 1024], "float32"),
+    "J": ("sbuf", [128, 1024], "float32"), "IN": ("sbuf", [128, 4], "float32"),
     "EB": ("sbuf", [128, 4], "float32"), "RB": ("sbuf", [128, 8], "float32"),
-    "SS": ("sbuf", [128, 8], "float32"), "MX": ("sbuf", [128, 8], "float32"),
+    "SS": ("sbuf", [128, 8], "float32"), "MX": ("sbuf", [128, 8], "float32"), "MR": ("sbuf", [128, 4], "float32"),
     "L1": ("sbuf", [128, 16], "float32"), "L2": ("sbuf", [128, 12], "float32"),
     "WB": ("sbuf", [128, 4], "float32"),
     "PS0": ("psum", [128, 512], "float32"), "PS1": ("psum", [128, 512], "float32"),
     "PS2": ("psum", [128, 512], "float32"), "PS3": ("psum", [128, 512], "float32"),
-    "PS4": ("psum", [128, 512], "float32"), "PS5": ("psum", [128, 512], "float32"),
-    "PS6": ("psum", [128, 512], "float32"), "PS7": ("psum", [128, 512], "float32"),
+    "PS4": ("psum", [128, 512], "float32"),
 }
-SEMAPHORES = (["le", "hl", "hr", "a1", "a2", "ls", "l1", "ys", "ss", "rl0", "rl1", "rl2", "rl3",
+SEMAPHORES = (["le", "hl", "hr", "a1", "a2", "ls", "l1", "lh", "cp", "ga", "ss", "rl0", "rl1", "rl2", "rl3",
                "lu0", "lu1", "lu2", "lb0", "lb1", "lb2"] + ["e%d" % i for i in range(NEV)])
 
 
@@ -38,6 +36,7 @@ def rank_program(g, core, T, topo):
     nev = [0]
     lsn = [0]
     l1n = [0]
+    lhn = [0]
 
     def ev():
         s = S["e%d" % nev[0]]
@@ -78,9 +77,9 @@ def rank_program(g, core, T, topo):
     def send(dst, out_ap, in_ap, rsem):
         rid, pid, _ = topo.addr(dst)
         m = topo.mask(core, dst)
-        g.remote_dma(out_ap=out_ap, in_ap=in_ap, remote_sem=rsem, local_sem=S.ls, pid=pid, routing_id=rid,
+        g.remote_dma(out_ap=out_ap, in_ap=in_ap, remote_sem=rsem, local_sem=S.lh, pid=pid, routing_id=rid,
                      dma_engine_mask=m)
-        lsn[0] += pc(m)
+        lhn[0] += pc(m)
 
     def fused(dsts, src, dst_aps, rsem, step1=False):
         m = topo.mask(core, dsts[0])
@@ -130,82 +129,112 @@ def rank_program(g, core, T, topo):
         if h[1] == core:
             hcount[h[2]] = pc(topo.mask(h[0] if h[3] is None else h[3], core))
 
-    CH = [(128, 256), (384, 256), (640, 256), (0, 128), (896, 128)]
-    PL = [((0, 0), (1, 0), (1, 256)), ((2, 0), (3, 0), (3, 256)), ((4, 0), (5, 0), (5, 256)),
-          ((6, 0), (6, 132), (6, 260)), ((7, 0), (7, 132), (7, 260))]
-    uload = [[(S.lu0, 16)], [(S.lu0, 16), (S.lu1, 16)], [(S.lu1, 16), (S.lu2, 16)],
-             [(S.lu0, 16), (S.hl, hcount["L"])], [(S.lu2, 16), (S.hr, hcount["R"])]]
-    bload = [(S.lb0, 16), (S.lb1, 16), (S.lb2, 16), (S.lb0, 16), (S.lb2, 16)]
-    VORD = "p0 p1 q0 r0 q1 p2 d0 r1 q2 m0 d1 r2 p3 p4 m1 d2 q3 q4 r3 r4 m2 d3 d4 m3 m4".split()
-    AORD = ("XP0 b40 b43 XP1 b41 pP0 b42 pP1 XP2 y0 b44 pP2 sq0 y1 XP3 XP4 sq1 y2 pP3 pP4 sq2 y3 y4 sq3 "
-            "sq4").split()
-    nk = len(CH)
-    done = dict(((op, k), ev()) for k in range(nk) for op in ("b4", "XP", "p", "pP", "q", "r", "y", "d", "m", "sq"))
-    s0 = 1.0 / math.sqrt(float(NR * WD))
+    SY.wait_ge(S.lh, lhn[0])
+    SY.dma_start(T.y[:, :], T.u[:, :]).then_inc(S.cp, 16)
 
-    def place(k, i, a, b):
-        bank, off = PL[k][i]
-        return T["PS%d" % bank][:, off + a:off + b]
+    CH = [(128, 256), (384, 256), (640, 256), (0, 128), (896, 128)]
+    uown = [[(S.lu0, 16)], [(S.lu0, 16), (S.lu1, 16)], [(S.lu1, 16), (S.lu2, 16)], [(S.lu0, 16)], [(S.lu2, 16)]]
+    bload = [(S.lb0, 16), (S.lb1, 16), (S.lb2, 16), (S.lb0, 16), (S.lb2, 16)]
+    VORD = "i0 i3 s0 s3 e0 s1 d0 e1 m0 d1 s2 m1 e2 h3 d2 s4 e3 m2 d3 e4 m3 d4 m4".split()
+    AORD = "b40 u90 b43 u93 b41 u91 sq0 c0 b42 u92 b44 u94 sq1 c1 sq2 c2 sq3 sq4 x0 c3 c4".split()
+    prev = {1: 0, 2: 1, 4: 2}
+    nk = len(CH)
+    done = dict(((op, k), ev()) for k in range(nk) for op in ("b4", "u9", "i", "h", "s", "e", "d", "m", "sq", "c"))
+    s0 = 1.0 / math.sqrt(float(NR * WD))
+    eMR, eMSG = ev(), ev()
+
+    def bank(k, i, w):
+        return T["PS%d" % k][:, 256 * i:256 * i + w]
 
     for name in VORD:
         op, k = name[:-1], int(name[-1])
         c0, w = CH[k]
-        o = PW * k
         cs = slice(c0, c0 + w)
-        if op == "p":
-            for sm, cnt in uload[k]:
+        if op == "i":
+            V.wait_ge(S.lu0, 16)
+            if k == 0:
+                ins = V.tensor_reduce(T.IN[:, 0:1], T.X[:, c0 - 1:c0 + 4], AX, ADD)
+            else:
+                ins = V.tensor_reduce(T.W5[:, 2:3], T.X[:, 2:7], AX, ADD)
+        elif op == "h":
+            V.wait_ge(S.hl, hcount["L"])
+            V.tensor_reduce(T.W5[:, 0:1], T.X[:, 0:5], AX, ADD).then_inc(done[("h", k)], 1)
+            ins = V.tensor_reduce(T.W5[:, 1:2], T.X[:, 1:6], AX, ADD)
+        elif op == "s":
+            for sm, cnt in uown[k]:
                 V.wait_ge(sm, cnt)
-            V.wait_ge(done[("XP", k)], 1)
-            if PL[k][2][0] == PL[k][0][0]:
-                V.wait_ge(done[("b4", k)], 1)
-            ins = V.tensor_tensor(T.P[:, o:o + w + 3], T.X[:, c0:c0 + w + 3], place(k, 0, 0, w + 3), ADD)
-        elif op == "q":
-            V.wait_ge(done[("p", k)], 1)
+            a = c0
+            if k == 0:
+                V.wait_ge(done[("i", 0)], 1)
+                init = T.IN[:, 0:1]
+            elif k == 3:
+                V.wait_ge(done[("i", 3)], 1)
+                init = T.W5[:, 2:3]
+                a = 3
+            else:
+                V.wait_ge(done[("s", prev[k])], 1)
+                init = T.W5[:, c0 - 1:c0]
+            if k == 4:
+                V.wait_ge(S.hr, hcount["R"])
+            z = c0 + w
+            ins = V.tensor_tensor_scan(T.W5[:, a:z], T.X[:, a + 4:z + 4], T.X[:, a - 1:z - 1], init, ADD, SUB)
+        elif op == "e":
+            V.wait_ge(done[("s", k)], 1)
+            if k == 3:
+                V.wait_ge(done[("h", 3)], 2)
             V.wait_ge(done[("b4", k)], 1)
-            V.wait_ge(done[("pP", k)], 1)
-            ins = V.tensor_tensor(T.Q[:, cs], T.P[:, o:o + w], place(k, 1, 0, w), ADD)
-        elif op == "r":
-            V.wait_ge(done[("q", k)], 1)
-            ins = V.tensor_tensor(T.R[:, cs], T.Q[:, cs], place(k, 2, 0, w), ADD)
+            V.wait_ge(done[("u9", k)], 1)
+            ins = V.tensor_tensor(T.E[:, cs], T.W5[:, cs], bank(k, 0, w), ADD)
         elif op == "d":
-            V.wait_ge(done[("y", k)], 1)
-            ins = V.tensor_tensor(T.D[:, cs], T.Y[:, cs], place(k, 0, 1, w + 1), SUB)
+            V.wait_ge(done[("e", k)], 1)
+            ins = V.tensor_tensor(T.D8[:, cs], T.E[:, cs], bank(k, 1, w), SUB)
         else:
             V.wait_ge(done[("d", k)], 1)
-            ins = V.tensor_reduce(T.MX[:, k:k + 1], T.D[:, cs], AX, MAX, apply_absolute_value=True)
+            ins = V.tensor_reduce(T.MX[:, k:k + 1], T.D8[:, cs], AX, MAX, apply_absolute_value=True)
         ins.then_inc(done[(op, k)], 1)
 
     for name in AORD:
         op, k = name[:-1], int(name[-1])
         c0, w = CH[k]
-        o = PW * k
         cs = slice(c0, c0 + w)
+        if op == "x":
+            SC.wait_ge(eZ, 2)
+            SC.wait_ge(eMR, 1)
+            SC.activation(T.L1[:, 4 * me + 2:4 * me + 3], T.MR[:, 0:1], COPY, scale=0.125).then_inc(eMSG, 1)
+            continue
         if op == "b4":
             SC.wait_ge(bload[k][0], bload[k][1])
-            ins = SC.activation(place(k, 2, 0, w), T.B[:, cs], COPY, scale=4.0)
-        elif op == "XP":
-            for sm, cnt in uload[k]:
+            ins = SC.activation(bank(k, 0, w), T.B[:, cs], COPY, scale=4.0)
+        elif op == "u9":
+            for sm, cnt in uown[k]:
                 SC.wait_ge(sm, cnt)
-            ins = SC.activation(place(k, 0, 0, w + 3), T.X[:, c0 + 1:c0 + w + 4], COPY)
-        elif op == "pP":
-            SC.wait_ge(done[("p", k)], 1)
-            ins = SC.activation(place(k, 1, 0, w), T.P[:, o + 3:o + w + 3], COPY)
-        elif op == "y":
-            SC.wait_ge(done[("r", k)], 1)
-            ins = SC.activation(T.Y[:, cs], T.R[:, cs], COPY, scale=0.125)
+            ins = SC.activation(bank(k, 1, w), T.X[:, c0 + 2:c0 + w + 2], COPY, scale=9.0)
+        elif op == "c":
+            SC.wait_ge(done[("d", k)], 1)
+            ins = SC.activation(T.D[:, cs], T.D8[:, cs], COPY, scale=0.125)
         else:
             SC.wait_ge(done[("d", k)], 1)
-            ins = SC.activation(T.J[:, cs], T.D[:, cs], SQUARE, scale=s0, accum_out=T.SS[:, k:k + 1])
+            ins = SC.activation(T.J[:, cs], T.D8[:, cs], SQUARE, scale=0.125 * s0, accum_out=T.SS[:, k:k + 1])
         ins.then_inc(done[(op, k)], 1)
 
-    eMSG = ev()
     V.wait_ge(eZ, 2)
     for k in range(nk):
         V.wait_ge(done[("m", k)], 1)
-    V.tensor_reduce(T.L1[:, 4 * me + 2:4 * me + 3], T.MX[:, 0:nk], AX, MAX).then_inc(eMSG, 1)
+    V.tensor_reduce(T.MR[:, 0:1], T.MX[:, 0:nk], AX, MAX).then_inc(eMR, 1)
     for k in range(nk):
         V.wait_ge(done[("sq", k)], 1)
     V.tensor_reduce(T.L1[:, 4 * me + 1:4 * me + 2], T.SS[:, 0:nk], AX, ADD).then_inc(eMSG, 1)
+
+    gan = [0]
+
+    def add_y(ks, a, b):
+        for k in ks:
+            g.wait_ge(done[("c", k)], 1)
+        g.dma_start(T.y[:, a:b], T.D[:, a:b], accum_op=ADD).then_inc(S.ga, 16)
+        gan[0] += 16
+
+    g.wait_ge(S.cp, 16)
+    add_y((0, 1), 128, 640)
 
     others = [c for c in peers if c != core]
     most = max(len(plan.get(c, [])) for c in peers)
@@ -216,6 +245,8 @@ def rank_program(g, core, T, topo):
     for grp in (first, rest):
         if grp:
             fused(grp, slot, [slot for _ in grp], S.a1, True)
+    add_y((2, 4), 640, 1024)
+    add_y((3,), 0, 128)
     V.wait_ge(eMSG, 2)
     V.wait_ge(S.a1, sum(pc(topo.mask(c, core)) for c in others))
     eC = ev()
@@ -232,6 +263,7 @@ def rank_program(g, core, T, topo):
         fused(plan[core], T.L2[:, 0:4], [slot2(topo.chip(core), d) for d in plan[core]], S.a2)
     g.wait_ge(S.ls, lsn[0])
     g.wait_ge(S.l1, l1n[0])
+    g.wait_ge(S.ga, gan[0])
 
     na2 = sum(pc(topo.mask(s, core)) for s in plan for d in plan[s] if d == core)
     V.wait_ge(eC, 2)
@@ -240,14 +272,6 @@ def rank_program(g, core, T, topo):
     V.tensor_reduce(T.WB[:, 1:2], T.L2[:, 1:12:4], AX, ADD).then_inc(eS, 1)
     V.tensor_reduce(T.WB[:, 2:3], T.L2[:, 2:12:4], AX, MAX).then_inc(eS, 1)
 
-    stores = [((0, 1), 128, 640), ((2,), 640, 896), ((3,), 0, 128), ((4,), 896, 1024)]
-    for i, (ks, a, b) in enumerate(stores):
-        for k in ks:
-            SY.wait_ge(done[("y", k)], 1)
-        if i == 2:
-            SY.wait_ge(S.l1, l1n[0])
-        SY.dma_start(T.y[:, a:b], T.Y[:, a:b]).then_inc(S.ys, 16)
-    SY.wait_ge(S.ys, 16 * len(stores))
     SC.wait_ge(eS, 2)
     SC.dma_start(T.s[:, :], T.WB[:, 1:3]).then_inc(S.ss, 16)
     SC.wait_ge(S.ss, 16)

import math
from concourse.bass import DstId, RemoteDMATransfer
from concourse.mybir import AluOpType, AxisListType, ActivationFunctionType

NR = 12
WD = 1024
NEV = 120

SCRATCH = {
    "X": ("sbuf", [128, 1028], "float32"), "B": ("sbuf", [128, 1024], "float32"),
    "W5": ("sbuf", [128, 1024], "float32"), "E": ("sbuf", [128, 1024], "float32"),
    "D8": ("sbuf", [128, 1024], "float32"), "D": ("sbuf", [128, 1024], "float32"),
    "J": ("sbuf", [128, 1024], "float32"), "IN": ("sbuf", [128, 4], "float32"),
    "EB": ("sbuf", [128, 4], "float32"), "RB": ("sbuf", [128, 8], "float32"),
    "SS": ("sbuf", [128, 8], "float32"), "MX": ("sbuf", [128, 8], "float32"), "MR": ("sbuf", [128, 4], "float32"),
    "L1": ("sbuf", [128, 16], "float32"), "L2": ("sbuf", [128, 12], "float32"),
    "WB": ("sbuf", [128, 4], "float32"),
    "PS0": ("psum", [128, 512], "float32"), "PS1": ("psum", [128, 512], "float32"),
    "PS2": ("psum", [128, 512], "float32"), "PS3": ("psum", [128, 512], "float32"),
    "PS4": ("psum", [128, 512], "float32"),
}
SEMAPHORES = (["le", "hl", "hr", "a1", "a2", "ls", "l1", "lh", "cp", "ga", "ss", "rl0", "rl1", "rl2", "rl3",
               "lu0", "lu1", "lu2", "lb0", "lb1", "lb2"] + ["e%d" % i for i in range(NEV)])


def rank_program(g, core, T, topo):
    cores = list(T.cores)
    n = len(cores)
    if core not in cores:
        return
    chips = sorted(set(topo.chip(c) for c in cores))
    V, SY, SC, S = g.vector, g.sync, g.scalar, T.sem
    ADD, SUB, MAX = AluOpType.add, AluOpType.subtract, AluOpType.max
    AX = AxisListType.X
    COPY, SQUARE = ActivationFunctionType.Copy, ActivationFunctionType.Square
    nev = [0]
    lsn = [0]
    l1n = [0]
    lhn = [0]

    def ev():
        s = S["e%d" % nev[0]]
        nev[0] += 1
        return s

    def pc(m):
        return bin(m).count("1")

    peers = [c for c in cores if topo.chip(c) == topo.chip(core)]
    me = peers.index(core)

    def relay_for(src, dst):
        if topo.may_write(src, dst):
            return None
        cand = [c for c in cores if c != src and c != dst and topo.chip(c) == topo.chip(src) and topo.may_write(c, dst)]
        same = [c for c in cand if topo.die(c) == topo.die(dst)]
        return (same or cand)[0]

    halo = []
    for r in range(n):
        halo.append((cores[r], cores[(r - 1) % n], "R", relay_for(cores[r], cores[(r - 1) % n])))
        halo.append((cores[r], cores[(r + 1) % n], "L", relay_for(cores[r], cores[(r + 1) % n])))
    jobs = [h for h in halo if h[3] is not None]

    plan = {}
    for ch in chips:
        mine = [c for c in cores if topo.chip(c) == ch]
        load = dict((c, 0) for c in mine)
        dsts = [d for d in cores if topo.chip(d) != ch]
        dsts.sort(key=lambda d: sum(1 for c in mine if topo.may_write(c, d)))
        for d in dsts:
            el = [c for c in mine if topo.may_write(c, d)]
            best = min(el, key=lambda c: (load[c], topo.die(c) != topo.die(d)))
            load[best] += 1
            plan.setdefault(best, []).append(d)

    def send(dst, out_ap, in_ap, rsem):
        rid, pid, _ = topo.addr(dst)
        m = topo.mask(core, dst)
        g.remote_dma(out_ap=out_ap, in_ap=in_ap, remote_sem=rsem, local_sem=S.lh, pid=pid, routing_id=rid,
                     dma_engine_mask=m)
        lhn[0] += pc(m)

    def fused(dsts, src, dst_aps, rsem, step1=False):
        m = topo.mask(core, dsts[0])
        for d in dsts:
            m &= topo.mask(core, d)
        ids = [DstId(rid=topo.addr(d)[0], pnc=topo.addr(d)[1]) for d in dsts]
        g.remote_dma_fused([RemoteDMATransfer(dst_ids=ids, dma_engine_mask=m, remote_sem=rsem, srcs=[src],
                                              dsts=dst_aps, alu_op=0)], local_sem=S.l1 if step1 else S.ls)
        (l1n if step1 else lsn)[0] += pc(m)

    def halo_ap(side):
        return (T.X[:, 1026:1028], S.hr) if side == "R" else (T.X[:, 0:2], S.hl)

    SY.dma_start(T.EB[:, 0:2], T.u[:, 1022:1024]).then_inc(S.le, 16)
    for i, (a, b) in enumerate([(0, 388), (388, 644), (644, 1024)]):
        SY.dma_start(T.X[:, a + 2:b + 2], T.u[:, a:b]).then_inc(S["lu%d" % i], 16)
    for i, (a, b) in enumerate([(0, 384), (384, 640), (640, 1024)]):
        SC.dma_start(T.B[:, a:b], T.b[:, a:b]).then_inc(S["lb%d" % i], 16)

    slot = T.L1[:, 4 * me:4 * me + 4]
    eZ = ev()
    V.memset(slot, 0.0).then_inc(eZ, 1)
    V.memset(T.L2[:, 0:4], 0.0).then_inc(eZ, 1)

    hcount = {}
    mysends = [h for h in halo if h[0] == core]
    mysends.sort(key=lambda h: h[2] == "R")
    for h in mysends:
        if h[2] == "R":
            g.wait_ge(S.lu0, 16)
            src_ap = T.X[:, 2:4]
        else:
            g.wait_ge(S.le, 16)
            src_ap = T.EB[:, 0:2]
        if h[3] is None:
            ap, sem = halo_ap(h[2])
            send(h[1], ap, src_ap, sem)
        else:
            j = jobs.index(h)
            send(h[3], T.RB[:, 2 * j:2 * j + 2], src_ap, S["rl%d" % j])
    for j, h in enumerate(jobs):
        if h[3] == core:
            g.wait_ge(S["rl%d" % j], pc(topo.mask(h[0], core)))
            ap, sem = halo_ap(h[2])
            send(h[1], ap, T.RB[:, 2 * j:2 * j + 2], sem)
    for h in halo:
        if h[1] == core:
            hcount[h[2]] = pc(topo.mask(h[0] if h[3] is None else h[3], core))

    SY.wait_ge(S.lh, lhn[0])
    SY.dma_start(T.y[:, :], T.u[:, :]).then_inc(S.cp, 16)

    CH = [(128, 256), (384, 256), (640, 256), (0, 128), (896, 128)]
    uown = [[(S.lu0, 16)], [(S.lu0, 16), (S.lu1, 16)], [(S.lu1, 16), (S.lu2, 16)], [(S.lu0, 16)], [(S.lu2, 16)]]
    bload = [(S.lb0, 16), (S.lb1, 16), (S.lb2, 16), (S.lb0, 16), (S.lb2, 16)]
    VORD = "i0 i3 s0 s3 e0 s1 d0 e1 m0 d1 s2 m1 e2 h3 d2 s4 e3 m2 d3 e4 m3 d4 m4".split()
    AORD = "b40 u90 b43 u93 b41 u91 sq0 c0 b42 u92 b44 u94 sq1 c1 sq2 c2 sq3 sq4 x0 c3 c4".split()
    prev = {1: 0, 2: 1, 4: 2}
    nk = len(CH)
    done = dict(((op, k), ev()) for k in range(nk) for op in ("b4", "u9", "i", "h", "s", "e", "d", "m", "sq", "c"))
    s0 = 1.0 / math.sqrt(float(NR * WD))
    eMR, eMSG = ev(), ev()

    def bank(k, i, w):
        return T["PS%d" % k][:, 256 * i:256 * i + w]

    for name in VORD:
        op, k = name[:-1], int(name[-1])
        c0, w = CH[k]
        cs = slice(c0, c0 + w)
        if op == "i":
            V.wait_ge(S.lu0, 16)
            if k == 0:
                ins = V.tensor_reduce(T.IN[:, 0:1], T.X[:, c0 - 1:c0 + 4], AX, ADD)
            else:
                ins = V.tensor_reduce(T.W5[:, 2:3], T.X[:, 2:7], AX, ADD)
        elif op == "h":
            V.wait_ge(S.hl, hcount["L"])
            V.tensor_reduce(T.W5[:, 0:1], T.X[:, 0:5], AX, ADD).then_inc(done[("h", k)], 1)
            ins = V.tensor_reduce(T.W5[:, 1:2], T.X[:, 1:6], AX, ADD)
        elif op == "s":
            for sm, cnt in uown[k]:
                V.wait_ge(sm, cnt)
            a = c0
            if k == 0:
                V.wait_ge(done[("i", 0)], 1)
                init = T.IN[:, 0:1]
            elif k == 3:
                V.wait_ge(done[("i", 3)], 1)
                init = T.W5[:, 2:3]
                a = 3
            else:
                V.wait_ge(done[("s", prev[k])], 1)
                init = T.W5[:, c0 - 1:c0]
            if k == 4:
                V.wait_ge(S.hr, hcount["R"])
            z = c0 + w
            ins = V.tensor_tensor_scan(T.W5[:, a:z], T.X[:, a + 4:z + 4], T.X[:, a - 1:z - 1], init, ADD, SUB)
        elif op == "e":
            V.wait_ge(done[("s", k)], 1)
            if k == 3:
                V.wait_ge(done[("h", 3)], 2)
            V.wait_ge(done[("b4", k)], 1)
            V.wait_ge(done[("u9", k)], 1)
            ins = V.tensor_tensor(T.E[:, cs], T.W5[:, cs], bank(k, 0, w), ADD)
        elif op == "d":
            V.wait_ge(done[("e", k)], 1)
            ins = V.tensor_tensor(T.D8[:, cs], T.E[:, cs], bank(k, 1, w), SUB)
        else:
            V.wait_ge(done[("d", k)], 1)
            ins = V.tensor_reduce(T.MX[:, k:k + 1], T.D8[:, cs], AX, MAX, apply_absolute_value=True)
        ins.then_inc(done[(op, k)], 1)

    for name in AORD:
        op, k = name[:-1], int(name[-1])
        c0, w = CH[k]
        cs = slice(c0, c0 + w)
        if op == "x":
            SC.wait_ge(eZ, 2)
            SC.wait_ge(eMR, 1)
            SC.activation(T.L1[:, 4 * me + 2:4 * me + 3], T.MR[:, 0:1], COPY, scale=0.125).then_inc(eMSG, 1)
            continue
        if op == "b4":
            SC.wait_ge(bload[k][0], bload[k][1])
            ins = SC.activation(bank(k, 0, w), T.B[:, cs], COPY, scale=4.0)
        elif op == "u9":
            for sm, cnt in uown[k]:
                SC.wait_ge(sm, cnt)
            ins = SC.activation(bank(k, 1, w), T.X[:, c0 + 2:c0 + w + 2], COPY, scale=9.0)
        elif op == "c":
            SC.wait_ge(done[("d", k)], 1)
            ins = SC.activation(T.D[:, cs], T.D8[:, cs], COPY, scale=0.125)
        else:
            SC.wait_ge(done[("d", k)], 1)
            ins = SC.activation(T.J[:, cs], T.D8[:, cs], SQUARE, scale=0.125 * s0, accum_out=T.SS[:, k:k + 1])
        ins.then_inc(done[(op, k)], 1)

    V.wait_ge(eZ, 2)
    for k in range(nk):
        V.wait_ge(done[("m", k)], 1)
    V.tensor_reduce(T.MR[:, 0:1], T.MX[:, 0:nk], AX, MAX).then_inc(eMR, 1)
    for k in range(nk):
        V.wait_ge(done[("sq", k)], 1)
    V.tensor_reduce(T.L1[:, 4 * me + 1:4 * me + 2], T.SS[:, 0:nk], AX, ADD).then_inc(eMSG, 1)

    gan = [0]

    def add_y(ks, a, b):
        for k in ks:
            g.wait_ge(done[("c", k)], 1)
        g.dma_start(T.y[:, a:b], T.D[:, a:b], accum_op=ADD).then_inc(S.ga, 16)
        gan[0] += 16

    g.wait_ge(S.cp, 16)
    add_y((0, 1), 128, 640)

    others = [c for c in peers if c != core]
    most = max(len(plan.get(c, [])) for c in peers)
    first = [c for c in others if len(plan.get(c, [])) == most]
    rest = [c for c in others if c not in first]
    g.wait_ge(eZ, 2)
    g.wait_ge(eMSG, 2)
    for grp in (first, rest):
        if grp:
            fused(grp, slot, [slot for _ in grp], S.a1, True)
    add_y((2, 4), 640, 1024)
    add_y((3,), 0, 128)
    V.wait_ge(eMSG, 2)
    V.wait_ge(S.a1, sum(pc(topo.mask(c, core)) for c in others))
    eC = ev()
    V.tensor_reduce(T.L2[:, 1:2], T.L1[:, 1:16:4], AX, ADD).then_inc(eC, 1)
    V.tensor_reduce(T.L2[:, 2:3], T.L1[:, 2:16:4], AX, MAX).then_inc(eC, 1)

    def slot2(src_chip, dst):
        oth = [x for x in chips if x != topo.chip(dst)]
        i = 1 + oth.index(src_chip)
        return T.L2[:, 4 * i:4 * i + 4]

    if core in plan:
        g.wait_ge(eC, 2)
        fused(plan[core], T.L2[:, 0:4], [slot2(topo.chip(core), d) for d in plan[core]], S.a2)
    g.wait_ge(S.ls, lsn[0])
    g.wait_ge(S.l1, l1n[0])
    g.wait_ge(S.ga, gan[0])

    na2 = sum(pc(topo.mask(s, core)) for s in plan for d in plan[s] if d == core)
    V.wait_ge(eC, 2)
    V.wait_ge(S.a2, na2)
    eS = ev()
    V.tensor_reduce(T.WB[:, 1:2], T.L2[:, 1:12:4], AX, ADD).then_inc(eS, 1)
    V.tensor_reduce(T.WB[:, 2:3], T.L2[:, 2:12:4], AX, MAX).then_inc(eS, 1)

    SC.wait_ge(eS, 2)
    SC.dma_start(T.s[:, :], T.WB[:, 1:3]).then_inc(S.ss, 16)
    SC.wait_ge(S.ss, 16)
